import numpy as np
import ml_dtypes


def mxq(x, axis, fmt="e4m3"):
    dtype, down = {"e4m3": (ml_dtypes.float8_e4m3fn, 7), "e5m2": (ml_dtypes.float8_e5m2, 14)}[fmt]
    v = np.moveaxis(np.asarray(x, np.float32).astype(ml_dtypes.bfloat16).astype(np.float64), axis, -1)
    blocks = v.reshape(v.shape[:-1] + (-1, 32))
    amax = np.abs(blocks).max(-1, keepdims=True)
    byte = np.maximum(np.where(amax > 0, np.frexp(amax)[1] - 1 + 127, 0) - down, 1)
    scale = np.exp2(byte - 127.0)
    codes = (blocks / scale).astype(np.float32).astype(dtype).astype(np.float64)
    return np.moveaxis((codes * scale).reshape(v.shape), -1, axis)


WIDE = False


def mx_kscale(k):
    if not WIDE:
        return np.ones(k)
    levels = np.array([10, -10, 5, -5, 0])
    if k % 512:
        return np.exp2(np.random.permutation(np.resize(levels, k // 32))).repeat(32)
    a = np.empty((k // 512, 16))
    for p in range(k // 512):
        a[p, :8] = np.random.permutation(np.resize(levels, 8))
        for g in range(8):
            far = levels[np.abs(levels - a[p, g]) >= 10]
            a[p, g + 8] = far[np.random.randint(len(far))]
    return np.exp2(a.ravel()).repeat(32)


def f64(x):
    return np.asarray(x).astype(np.float64)


def striped(idx):
    return np.tile(idx.reshape(-1, 16).T, (8, 1)).astype(np.uint16)


def unstriped(offs):
    return offs[:16].T.reshape(-1).astype(np.int64)


E2M1 = np.array([0.0, 0.5, 1.0, 1.5, 2.0, 3.0, 4.0, 6.0, -0.0, -0.5, -1.0, -1.5, -2.0, -3.0, -4.0, -6.0])


def pack_weight(w, fmt):
    k, n = w.shape
    w = f64(np.asarray(w, np.float32).astype(ml_dtypes.bfloat16)).reshape(k // 32, 32, n)
    amax = np.abs(w).max(1)
    if fmt == "e4m3":
        byte = np.frexp(amax)[1] - 1 + 127 - 7
    else:
        mant, ex = np.frexp(amax / 6.0)
        byte = np.where(mant > 0.5, ex, ex - 1) + 127
    byte = np.clip(np.where(amax > 0, byte, 1), 1, 254)
    scaled = (w * np.exp2(127.0 - byte)[:, None, :]).reshape(k, n).astype(np.float32)
    by_word = np.ascontiguousarray(scaled.reshape(k // 512, 128, 4, n).transpose(0, 1, 3, 2))
    if fmt == "e4m3":
        words = by_word.astype(ml_dtypes.float8_e4m3fn).view(np.uint8)
    else:
        c = by_word.astype(ml_dtypes.float4_e2m1fn).view(np.uint8) & 0xF
        words = (c[..., 0::2] | (c[..., 1::2] << 4)).reshape(k // 512, 128, 2 * n)
    return np.ascontiguousarray(words), np.ascontiguousarray(byte.astype(np.uint8).reshape(k // 512, 16, n))


def unpack_weight(words, scales, fmt):
    g, _, n = scales.shape
    words = np.ascontiguousarray(words).reshape(g, 128, n, -1)
    if fmt == "e4m3":
        vals = words.view(ml_dtypes.float8_e4m3fn).astype(np.float64)
    else:
        nib = np.empty((g, 128, n, 4), np.uint8)
        nib[..., 0::2] = words & 0xF
        nib[..., 1::2] = words >> 4
        vals = E2M1[nib]
    vals = vals * np.repeat(np.exp2(scales.astype(np.float64) - 127.0), 8, axis=1)[..., None]
    return vals.transpose(0, 1, 3, 2).reshape(g * 512, n)


def gelu(v):
    return 0.5 * v * (1.0 + np.tanh(np.sqrt(2.0 / np.pi) * (v + 0.044715 * v**3)))


K, T, S, H, N = 1536, 2048, 1024, 1024, 512

def setup_inputs():
    n = np.random.standard_normal
    s = mx_kscale(K)[:, None]
    u = mx_kscale(H)[:, None]
    tab_words, tab_scales = pack_weight(n((K, T)) * s, "e4m3")
    w4_words, w4_scales = pack_weight(n((K, H)) / np.sqrt(K) / s * u.T, "e2m1")
    w2 = (2.0 * n((H, N)) / np.sqrt(H) / u).astype(np.float32)
    gT = (1.5 * n((N, T))).astype(np.float32)
    offs = striped(np.random.permutation(T)[:S])
    return {"tab_words": tab_words, "tab_scales": tab_scales, "offs": offs,
            "w4_words": w4_words, "w4_scales": w4_scales, "w2": w2, "gT": gT}

def reference(tab_words, tab_scales, offs, w4_words, w4_scales, w2, gT):
    v = unpack_weight(tab_words, tab_scales, "e4m3")[:, unstriped(offs)]
    g = f64(gT)[:, unstriped(offs)]
    w4 = unpack_weight(w4_words, w4_scales, "e2m1")
    h = np.maximum(w4.T @ v, 0.0)
    p = mxq(f64(w2), 0, "e4m3").T @ mxq(h, 0, "e4m3")
    r = p - g
    return np.sqrt(1.0 + r * r) - 1.0

@@ -1,0 +1,244 @@
+from contextlib import ExitStack
+
+import concourse.mybir as mybir
+
+K, T, S, H, N = 1536, 2048, 1024, 1024, 512
+FLOPS = 2 * K * H * S + 2 * H * N * S
+
+F32 = mybir.dt.float32
+BF16 = mybir.dt.bfloat16
+I32 = mybir.dt.int32
+U32 = mybir.dt.uint32
+U16 = mybir.dt.uint16
+U8 = mybir.dt.uint8
+FP8X4 = mybir.dt.float8_e4m3fn_x4
+FP4X4 = mybir.dt.float4_e2m1fn_x4
+ACT = mybir.ActivationFunctionType
+ALU = mybir.AluOpType
+
+P = 128
+KP = K // 512
+HP = H // 512
+NT = N // P
+MOVE_ROWS = 112
+KIB = 1024
+CAST = ["scalar","scalar"]
+MINUS = ["vector","vector","vector","vector","vector","vector","vector","vector"]
+
+
+def tile_list_pseudo_huber_reprojection_kernel(tc, tab_words, tab_scales, offs, w4_words, w4_scales, w2, gT, out):
+    nc = tc.nc
+    with ExitStack() as ctx:
+        held = ctx.enter_context(tc.tile_pool(name="held", bufs=1))
+        shared = ctx.enter_context(tc.tile_pool(name="shared", bufs=1))
+        psum = ctx.enter_context(tc.psum_pool(name="psum", bufs=1))
+
+        def placed(name, shape, dtype, offset):
+            return shared.tile(shape, dtype, name=name, offset=offset, align_bytes=64)
+
+        def kept(name, shape, dtype):
+            return held.tile(shape, dtype, name=name, align_bytes=64)
+
+        offsets = held.tile([P, S // 16], U16, name="offsets")
+        nc.sync.dma_start(offsets[:], offs)
+
+        def picks(j0, j1):
+            return offsets[:, j0 // 16 : j1 // 16]
+
+        scale_win = placed("scale_win", [P, T // 4], I32, 4 * KIB)
+        nc.vector.memset(scale_win[:], 0)
+        for q in range(4):
+            nc.scalar.dma_start(scale_win[32 * q : 32 * q + 4 * KP, :], tab_scales[:, 4 * q : 4 * q + 4, :].bitcast(I32))
+        w4s_raw = placed("w4s_raw", [P, KP, H // 4], I32, 29 * KIB)
+        nc.gpsimd.memset(w4s_raw[:], 0)
+        for q in range(4):
+            nc.gpsimd.dma_start(w4s_raw[32 * q : 32 * q + 4, :, :],
+                                w4_scales[:, 4 * q : 4 * q + 4, :].rearrange("a r c -> r a c").bitcast(I32))
+        moved = kept("moved", [P, KP - 1, S // 4], I32)
+        nc.vector.memset(moved[:], 0)
+        one = kept("one", [P, 1], F32)
+        nc.vector.memset(one[:], 1.0)
+        minus_one = kept("minus_one", [P, 1], F32)
+        nc.vector.memset(minus_one[:], -1.0)
+        warm = kept("warm", [P, 1], F32)
+        nc.scalar.activation(out=warm[:], in_=one[:], func=ACT.Sqrt, bias=one[:])
+
+        tab_win = [placed("tab_win%d" % a, [P, T], I32, (34, 46, 58)[a] * KIB) for a in range(KP)]
+        w4_raw = placed("w4_raw", [P, KP, H // 2], I32, 6 * KIB)
+
+        def load_tab(a):
+            nc.sync.dma_start(tab_win[a][:], tab_words[a].rearrange("p t i -> p (t i)").bitcast(I32))
+
+        load_tab(0)
+        nc.sync.dma_start(w4_raw[:], w4_words.rearrange("a p c -> p a c").bitcast(I32))
+        load_tab(1)
+        load_tab(2)
+
+        v_tiles = []
+
+        def gather_tab(a, j0, j1, offset):
+            name = "v%d_%d" % (a, j0)
+            tile = kept(name, [P, j1 - j0], U32) if offset is None else placed(name, [P, j1 - j0], U32, offset)
+            v_tiles.append((a, j0, j1, tile))
+            nc.vector.tensor_copy(tile[:], tab_win[a][:].bitcast(U32).indirect(picks(j0, j1)))
+
+        def v_cols(a, j0, j1):
+            for pass_, lo, hi, tile in v_tiles:
+                if pass_ == a and lo <= j0 and j1 <= hi:
+                    return tile[:, j0 - lo : j1 - lo]
+            raise ValueError("no tile")
+
+        gather_tab(0, 0, 512, None)
+        v_scales = kept("v_scales", [P, S], U8)
+        nc.vector.tensor_copy(v_scales[:], scale_win[:].bitcast(U8).indirect(picks(0, S)))
+        for a in range(1, KP):
+            nc.scalar.dma_start(moved[0:MOVE_ROWS, a - 1, :], v_scales[4 * a : 4 * a + MOVE_ROWS, :].bitcast(I32))
+        gather_tab(0, 512, 1024, None)
+
+        def v_plane(a, j0, j1):
+            if a == 0:
+                return v_scales[:, j0:j1]
+            return moved[:, a - 1, j0 // 4 : j1 // 4].bitcast(U8)
+
+        w4_codes = placed("w4_codes", [P, KP, H // 2], I32, 0)
+        for a in range(KP):
+            nc.vector.tensor_copy(w4_codes[:, a, :].rearrange("p (b t q w) -> p b t q w", b=HP, t=4, q=16),
+                                  w4_raw[:, a, :].rearrange("p (b q t w) -> p b t q w", b=HP, t=4, q=16))
+        gather_tab(1, 0, 512, 6 * KIB)
+        w4_planes = placed("w4_planes", [P, KP, H // 4], I32, 8 * KIB)
+        nc.vector.tensor_copy(w4_planes[:].rearrange("p a (b t q w) -> p (a b) t q w", b=HP, t=4, q=16),
+                              w4s_raw[:].rearrange("p a (b q t w) -> p (a b) t q w", b=HP, t=4, q=16))
+        gather_tab(2, 0, 256, 29 * KIB + 64)
+        gather_tab(2, 256, 512, 30 * KIB + 64)
+        gather_tab(1, 512, 1024, 27 * KIB + 64)
+        gather_tab(2, 512, 1024, 31 * KIB + 64)
+
+        g_win = [placed("g_win%d" % m, [P, T], F32, (34, 42, 50, 58)[m] * KIB) for m in range(NT)]
+
+        def load_g(m):
+            nc.sync.dma_start(g_win[m][:], gT[P * m : P * (m + 1), :])
+
+        load_g(0)
+        w2_raw = placed("w2_raw", [P, 4 * HP, N], F32, 11 * KIB)
+        w2_rows = w2.rearrange("(b q t i) n -> b t q i n", b=HP, q=16, t=4)
+        for b in range(HP):
+            for t in range(4):
+                nc.sync.dma_start(w2_raw[:, 4 * b + t, :], w2_rows[b, t])
+        for m in range(1, NT):
+            load_g(m)
+
+        h_codes = kept("h_codes", [P, HP, S], U32)
+        h_scales = kept("h_scales", [P, HP, S], U8)
+        turn = [0]
+
+        def decode(b, j0, j1, offset):
+            name = "h%d_%d" % (b, j0)
+            shape = [P, j1 - j0, 4]
+            grouped = kept(name, shape, BF16) if offset is None else placed(name, shape, BF16, offset)
+            for j in range(j0, j1, P):
+                bank = psum.tile([P, 4, P], F32, name="decode_bank", tag="bank%d" % (turn[0] % 4))
+                turn.append(turn.pop() + 1)
+                for t in range(4):
+                    for a in range(KP):
+                        nc.tensor.matmul_mx(
+                            out=bank[:, t, :],
+                            lhsT=w4_codes[:, a, 256 * b + 64 * t : 256 * b + 64 * (t + 1)].bitcast(U8).bitcast(FP4X4),
+                            lhsT_scale=w4_planes[:, a, 128 * b + 32 * t : 128 * b + 32 * (t + 1)].bitcast(U8),
+                            rhs=v_cols(a, j, j + P).bitcast(FP8X4),
+                            rhs_scale=v_plane(a, j, j + P),
+                            start=(a == 0),
+                            stop=(a == KP - 1),
+                        )
+                nc.scalar.activation(out=grouped[:, j - j0 : j - j0 + P, :], in_=bank[:].rearrange("p t j -> p j t"), func=ACT.Relu)
+            nc.vector.quantize_mx(out=h_codes[:, b, j0:j1].bitcast(FP8X4), scales=h_scales[:, b, j0:j1],
+                                  in_=grouped[:].rearrange("p j t -> p (j t)"))
+
+        w2_codes = kept("w2_codes", [P, HP, N], U32)
+        w2_scales = kept("w2_scales", [P, HP, N], U8)
+
+        def quantize_w2(b):
+            grouped = placed("w2_grouped%d" % b, [P, N, 4], BF16, (67, 75)[b] * KIB)
+            step = N if CAST[b] == "vector" else P
+            for n0 in range(0, N, step):
+                dst = grouped[:, n0 : n0 + step, :].rearrange("p (c i) t -> p c t i", i=4)
+                src = w2_raw[:, 4 * b : 4 * b + 4, n0 : n0 + step].rearrange("p t (c i) -> p c t i", i=4)
+                if CAST[b] == "vector":
+                    nc.vector.tensor_copy(dst, src)
+                elif CAST[b] == "gpsimd":
+                    nc.gpsimd.tensor_scalar(dst, src, 1.0, 0.0, ALU.mult, ALU.add)
+                else:
+                    nc.scalar.copy(dst, src)
+            nc.vector.quantize_mx(out=w2_codes[:, b, :].bitcast(FP8X4), scales=w2_scales[:, b, :],
+                                  in_=grouped[:].rearrange("p n t -> p (n t)"))
+
+        g_tiles = []
+
+        def gather_g(m, j0, j1, offset):
+            tile = placed("g%d_%d" % (m, j0), [P, j1 - j0], F32, offset)
+            g_tiles.append((m, j0, j1, tile))
+            nc.vector.tensor_copy(tile[:], g_win[m][:].indirect(picks(j0, j1)))
+
+        def g_cols(m, j0, j1):
+            for row, lo, hi, tile in g_tiles:
+                if row == m and lo <= j0 and j1 <= hi:
+                    return tile[:, j0 - lo : j1 - lo]
+            raise ValueError("no tile")
+
+        out_rows = out.rearrange("(m p) j -> p m j", p=P)
+        unit = [0]
+
+        def project(m0, m1, j0, j1):
+            u = unit.pop()
+            unit.append(u + 1)
+            bank = psum.tile([P, m1 - m0, j1 - j0], F32, name="project_bank", tag="bank%d" % (4 + u % 4))
+            for m in range(m0, m1):
+                for b in range(HP):
+                    nc.tensor.matmul_mx(
+                        out=bank[:, m - m0, :],
+                        lhsT=w2_codes[:, b, P * m : P * (m + 1)].bitcast(FP8X4),
+                        lhsT_scale=w2_scales[:, b, P * m : P * (m + 1)],
+                        rhs=h_codes[:, b, j0:j1].bitcast(FP8X4),
+                        rhs_scale=h_scales[:, b, j0:j1],
+                        start=(b == 0),
+                        stop=(b == HP - 1),
+                    )
+            res = kept("res%d" % u, [P, m1 - m0, j1 - j0], F32)
+            for m in range(m0, m1):
+                nc.vector.tensor_tensor(res[:, m - m0, :], bank[:, m - m0, :], g_cols(m, j0, j1), ALU.subtract)
+            nc.scalar.activation(out=res[:], in_=res[:], func=ACT.Square)
+            nc.scalar.activation(out=res[:], in_=res[:], func=ACT.Sqrt, bias=one[:])
+            if MINUS[u] == "vector":
+                nc.vector.tensor_scalar(res[:], res[:], 1.0, -1.0, ALU.mult, ALU.add)
+            elif MINUS[u] == "gpsimd":
+                nc.gpsimd.tensor_scalar(res[:], res[:], 1.0, -1.0, ALU.mult, ALU.add)
+            else:
+                nc.scalar.activation(out=res[:], in_=res[:], func=ACT.Identity, bias=minus_one[:])
+            nc.sync.dma_start(out_rows[:, m0:m1, j0:j1], res[:])
+
+        decode(0, 0, 256, 70 * KIB)
+        decode(1, 0, 256, 78 * KIB)
+        quantize_w2(0)
+        gather_g(0, 0, 1024, 71 * KIB)
+        decode(0, 256, 512, 80 * KIB)
+        quantize_w2(1)
+        decode(1, 256, 512, 82 * KIB)
+        gather_g(1, 0, 512, 80 * KIB)
+        decode(0, 512, 768, 84 * KIB)
+        project(0, 1, 0, 512)
+        gather_g(2, 0, 512, 82 * KIB)
+        decode(1, 512, 768, None)
+        project(1, 2, 0, 512)
+        gather_g(1, 512, 1024, 84 * KIB)
+        decode(0, 768, 896, None)
+        decode(1, 768, 896, None)
+        project(2, 3, 0, 512)
+        gather_g(3, 0, 512, 80 * KIB)
+        decode(0, 896, 1024, None)
+        decode(1, 896, 1024, None)
+        project(0, 2, 512, 768)
+        gather_g(2, 512, 1024, 82 * KIB)
+        project(3, 4, 0, 512)
+        gather_g(3, 512, 1024, 80 * KIB)
+        project(2, 4, 512, 768)
+        project(0, 4, 768, 896)
+        project(0, 4, 896, 1024)

@@ -22,7 +22,7 @@ HP = H // 512
 NT = N // P
 MOVE_ROWS = 112
 KIB = 1024
-CAST = ["scalar","scalar"]
+CAST = ["vector","scalar"]
 MINUS = ["vector","vector","vector","vector","vector","vector","vector","vector"]
 
 
@@ -45,34 +45,33 @@ def tile_list_pseudo_huber_reprojection_kernel(tc, tab_words, tab_scales, offs, 
         def picks(j0, j1):
             return offsets[:, j0 // 16 : j1 // 16]
 
-        scale_win = placed("scale_win", [P, T // 4], I32, 4 * KIB)
-        nc.vector.memset(scale_win[:], 0)
-        for q in range(4):
-            nc.scalar.dma_start(scale_win[32 * q : 32 * q + 4 * KP, :], tab_scales[:, 4 * q : 4 * q + 4, :].bitcast(I32))
-        w4s_raw = placed("w4s_raw", [P, KP, H // 4], I32, 29 * KIB)
-        nc.gpsimd.memset(w4s_raw[:], 0)
-        for q in range(4):
-            nc.gpsimd.dma_start(w4s_raw[32 * q : 32 * q + 4, :, :],
-                                w4_scales[:, 4 * q : 4 * q + 4, :].rearrange("a r c -> r a c").bitcast(I32))
-        moved = kept("moved", [P, KP - 1, S // 4], I32)
-        nc.vector.memset(moved[:], 0)
-        one = kept("one", [P, 1], F32)
-        nc.vector.memset(one[:], 1.0)
-        minus_one = kept("minus_one", [P, 1], F32)
-        nc.vector.memset(minus_one[:], -1.0)
-        warm = kept("warm", [P, 1], F32)
-        nc.scalar.activation(out=warm[:], in_=one[:], func=ACT.Sqrt, bias=one[:])
-
-        tab_win = [placed("tab_win%d" % a, [P, T], I32, (34, 46, 58)[a] * KIB) for a in range(KP)]
-        w4_raw = placed("w4_raw", [P, KP, H // 2], I32, 6 * KIB)
+        tab_win = [placed("tab_win%d" % a, [P, T], I32, (46, 58, 70)[a] * KIB) for a in range(KP)]
 
         def load_tab(a):
             nc.sync.dma_start(tab_win[a][:], tab_words[a].rearrange("p t i -> p (t i)").bitcast(I32))
 
         load_tab(0)
+        scale_win = placed("scale_win", [P, T // 4], I32, 5 * KIB)
+        nc.vector.memset(scale_win[:], 0)
+        for q in range(4):
+            queue = nc.scalar if q % 2 else nc.sync
+            queue.dma_start(scale_win[32 * q : 32 * q + 4 * KP, :], tab_scales[:, 4 * q : 4 * q + 4, :].bitcast(I32))
+        w4_raw = placed("w4_raw", [P, KP, H // 2], I32, 24 * KIB)
         nc.sync.dma_start(w4_raw[:], w4_words.rearrange("a p c -> p a c").bitcast(I32))
+        w4s_raw = placed("w4s_raw", [P, KP, H // 4], I32, 116 * KIB)
+        nc.vector.memset(w4s_raw[:], 0)
+        for q in range(4):
+            nc.sync.dma_start(w4s_raw[32 * q : 32 * q + 4, :, :],
+                              w4_scales[:, 4 * q : 4 * q + 4, :].rearrange("a r c -> r a c").bitcast(I32))
         load_tab(1)
         load_tab(2)
+        moved = kept("moved", [P, KP - 1, S // 4], I32)
+        nc.vector.memset(moved[:], 0)
+        one = kept("one", [P, 1], F32)
+        nc.vector.memset(one[:], 1.0)
+        minus_one = one
+        warm = kept("warm", [P, 1], F32)
+        nc.scalar.activation(out=warm[:], in_=one[:], func=ACT.Sqrt, bias=one[:])
 
         v_tiles = []
 
@@ -92,8 +91,7 @@ def tile_list_pseudo_huber_reprojection_kernel(tc, tab_words, tab_scales, offs, 
         v_scales = kept("v_scales", [P, S], U8)
         nc.vector.tensor_copy(v_scales[:], scale_win[:].bitcast(U8).indirect(picks(0, S)))
         for a in range(1, KP):
-            nc.scalar.dma_start(moved[0:MOVE_ROWS, a - 1, :], v_scales[4 * a : 4 * a + MOVE_ROWS, :].bitcast(I32))
-        gather_tab(0, 512, 1024, None)
+            (nc.scalar, nc.sync)[a - 1].dma_start(moved[0:MOVE_ROWS, a - 1, :], v_scales[4 * a : 4 * a + MOVE_ROWS, :].bitcast(I32))
 
         def v_plane(a, j0, j1):
             if a == 0:
@@ -104,26 +102,27 @@ def tile_list_pseudo_huber_reprojection_kernel(tc, tab_words, tab_scales, offs, 
         for a in range(KP):
             nc.vector.tensor_copy(w4_codes[:, a, :].rearrange("p (b t q w) -> p b t q w", b=HP, t=4, q=16),
                                   w4_raw[:, a, :].rearrange("p (b q t w) -> p b t q w", b=HP, t=4, q=16))
-        gather_tab(1, 0, 512, 6 * KIB)
-        w4_planes = placed("w4_planes", [P, KP, H // 4], I32, 8 * KIB)
+        gather_tab(1, 0, 512, 24 * KIB + 64)
+        w4_planes = placed("w4_planes", [P, KP, H // 4], I32, 26 * KIB + 64)
         nc.vector.tensor_copy(w4_planes[:].rearrange("p a (b t q w) -> p (a b) t q w", b=HP, t=4, q=16),
                               w4s_raw[:].rearrange("p a (b q t w) -> p (a b) t q w", b=HP, t=4, q=16))
-        gather_tab(2, 0, 256, 29 * KIB + 64)
-        gather_tab(2, 256, 512, 30 * KIB + 64)
-        gather_tab(1, 512, 1024, 27 * KIB + 64)
-        gather_tab(2, 512, 1024, 31 * KIB + 64)
+        gather_tab(2, 0, 256, 116 * KIB + 64)
+        gather_tab(2, 256, 512, 117 * KIB + 64)
+        gather_tab(2, 512, 1024, 118 * KIB + 64)
+        gather_tab(1, 512, 1024, 72 * KIB)
+        gather_tab(0, 512, 1024, 70 * KIB)
 
-        g_win = [placed("g_win%d" % m, [P, T], F32, (34, 42, 50, 58)[m] * KIB) for m in range(NT)]
+        g_win = [placed("g_win%d" % m, [P, T], F32, (29 * KIB + 64, 54 * KIB, 62 * KIB, 46 * KIB)[m]) for m in range(NT)]
 
         def load_g(m):
             nc.sync.dma_start(g_win[m][:], gT[P * m : P * (m + 1), :])
 
         load_g(0)
-        w2_raw = placed("w2_raw", [P, 4 * HP, N], F32, 11 * KIB)
+        w2_raw = placed("w2_raw", [P, 4 * HP, N], F32, 100 * KIB + 64)
         w2_rows = w2.rearrange("(b q t i) n -> b t q i n", b=HP, q=16, t=4)
         for b in range(HP):
             for t in range(4):
-                nc.sync.dma_start(w2_raw[:, 4 * b + t, :], w2_rows[b, t])
+                nc.scalar.dma_start(w2_raw[:, 4 * b + t, :], w2_rows[b, t])
         for m in range(1, NT):
             load_g(m)
 
@@ -157,11 +156,11 @@ def tile_list_pseudo_huber_reprojection_kernel(tc, tab_words, tab_scales, offs, 
         w2_scales = kept("w2_scales", [P, HP, N], U8)
 
         def quantize_w2(b):
-            grouped = placed("w2_grouped%d" % b, [P, N, 4], BF16, (67, 75)[b] * KIB)
+            grouped = placed("w2_grouped%d" % b, [P, N, 4], BF16, (79, 87)[b] * KIB)
             step = N if CAST[b] == "vector" else P
             for n0 in range(0, N, step):
-                dst = grouped[:, n0 : n0 + step, :].rearrange("p (c i) t -> p c t i", i=4)
-                src = w2_raw[:, 4 * b : 4 * b + 4, n0 : n0 + step].rearrange("p t (c i) -> p c t i", i=4)
+                dst = grouped[:, n0 : n0 + step, :]
+                src = w2_raw[:, 4 * b : 4 * b + 4, n0 : n0 + step].rearrange("p t n -> p n t")
                 if CAST[b] == "vector":
                     nc.vector.tensor_copy(dst, src)
                 elif CAST[b] == "gpsimd":
@@ -174,7 +173,8 @@ def tile_list_pseudo_huber_reprojection_kernel(tc, tab_words, tab_scales, offs, 
         g_tiles = []
 
         def gather_g(m, j0, j1, offset):
-            tile = placed("g%d_%d" % (m, j0), [P, j1 - j0], F32, offset)
+            name = "g%d_%d" % (m, j0)
+            tile = kept(name, [P, j1 - j0], F32) if offset is None else placed(name, [P, j1 - j0], F32, offset)
             g_tiles.append((m, j0, j1, tile))
             nc.vector.tensor_copy(tile[:], g_win[m][:].indirect(picks(j0, j1)))
 
@@ -215,30 +215,31 @@ def tile_list_pseudo_huber_reprojection_kernel(tc, tab_words, tab_scales, offs, 
                 nc.scalar.activation(out=res[:], in_=res[:], func=ACT.Identity, bias=minus_one[:])
             nc.sync.dma_start(out_rows[:, m0:m1, j0:j1], res[:])
 
-        decode(0, 0, 256, 70 * KIB)
-        decode(1, 0, 256, 78 * KIB)
+        decode(0, 0, 256, 82 * KIB)
+        decode(1, 0, 256, 90 * KIB)
         quantize_w2(0)
-        gather_g(0, 0, 1024, 71 * KIB)
-        decode(0, 256, 512, 80 * KIB)
+        gather_g(0, 0, 512, 78912)
+        decode(0, 256, 512, 126 * KIB)
         quantize_w2(1)
-        decode(1, 256, 512, 82 * KIB)
-        gather_g(1, 0, 512, 80 * KIB)
-        decode(0, 512, 768, 84 * KIB)
+        decode(1, 256, 512, 132 * KIB)
+        gather_g(0, 512, 1024, 127040)
+        decode(0, 512, 768, 138 * KIB)
         project(0, 1, 0, 512)
-        gather_g(2, 0, 512, 82 * KIB)
-        decode(1, 512, 768, None)
+        gather_g(1, 0, 512, 133184)
+        decode(1, 512, 768, 144 * KIB)
         project(1, 2, 0, 512)
-        gather_g(1, 512, 1024, 84 * KIB)
-        decode(0, 768, 896, None)
-        decode(1, 768, 896, None)
+        gather_g(1, 512, 1024, 78912)
+        gather_g(2, 0, 512, 139328)
+        decode(0, 768, 896, 150 * KIB)
+        decode(1, 768, 896, 156 * KIB)
         project(2, 3, 0, 512)
-        gather_g(3, 0, 512, 80 * KIB)
-        decode(0, 896, 1024, None)
-        decode(1, 896, 1024, None)
+        gather_g(2, 512, 1024, 133184)
+        gather_g(3, 0, 512, 145472)
         project(0, 2, 512, 768)
-        gather_g(2, 512, 1024, 82 * KIB)
+        decode(0, 896, 1024, 162 * KIB)
+        decode(1, 896, 1024, None)
         project(3, 4, 0, 512)
-        gather_g(3, 512, 1024, 80 * KIB)
+        gather_g(3, 512, 1024, 139328)
         project(2, 4, 512, 768)
         project(0, 4, 768, 896)
         project(0, 4, 896, 1024)

@@ -21,9 +21,10 @@ KP = K // 512
 HP = H // 512
 NT = N // P
 MOVE_ROWS = 112
+HALF = S // 2
+QUARTER = S // 4
 KIB = 1024
-CAST = ["vector","scalar"]
-MINUS = ["vector","vector","vector","vector","vector","vector","vector","vector"]
+BANKS = 8
 
 
 def tile_list_pseudo_huber_reprojection_kernel(tc, tab_words, tab_scales, offs, w4_words, w4_scales, w2, gT, out):
@@ -33,11 +34,10 @@ def tile_list_pseudo_huber_reprojection_kernel(tc, tab_words, tab_scales, offs, 
         shared = ctx.enter_context(tc.tile_pool(name="shared", bufs=1))
         psum = ctx.enter_context(tc.psum_pool(name="psum", bufs=1))
 
-        def placed(name, shape, dtype, offset):
+        def tile(name, shape, dtype, offset=None):
+            if offset is None:
+                return held.tile(shape, dtype, name=name, align_bytes=64)
             return shared.tile(shape, dtype, name=name, offset=offset, align_bytes=64)
-
-        def kept(name, shape, dtype):
-            return held.tile(shape, dtype, name=name, align_bytes=64)
 
         offsets = held.tile([P, S // 16], U16, name="offsets")
         nc.sync.dma_start(offsets[:], offs)
@@ -45,201 +45,200 @@ def tile_list_pseudo_huber_reprojection_kernel(tc, tab_words, tab_scales, offs, 
         def picks(j0, j1):
             return offsets[:, j0 // 16 : j1 // 16]
 
-        tab_win = [placed("tab_win%d" % a, [P, T], I32, (46, 58, 70)[a] * KIB) for a in range(KP)]
-
-        def load_tab(a):
-            nc.sync.dma_start(tab_win[a][:], tab_words[a].rearrange("p t i -> p (t i)").bitcast(I32))
-
-        load_tab(0)
-        scale_win = placed("scale_win", [P, T // 4], I32, 5 * KIB)
+        scale_win = tile("scale_win", [P, T // 4], I32)
         nc.vector.memset(scale_win[:], 0)
+        w4s_raw = tile("w4s_raw", [P, KP, H // 4], I32, 0)
+        nc.vector.memset(w4s_raw[:], 0)
+        moved = tile("moved", [P, KP - 1, S // 4], I32)
+        nc.vector.memset(moved[:], 0)
+        unit = tile("unit", [P, 1], F32)
+        nc.vector.memset(unit[:], 1.0)
+        w4_raw = tile("w4_raw", [P, KP, H // 2], I32)
+        nc.sync.dma_start(w4_raw[:], w4_words.rearrange("a p c -> p a c").bitcast(I32))
         for q in range(4):
             queue = nc.scalar if q % 2 else nc.sync
             queue.dma_start(scale_win[32 * q : 32 * q + 4 * KP, :], tab_scales[:, 4 * q : 4 * q + 4, :].bitcast(I32))
-        w4_raw = placed("w4_raw", [P, KP, H // 2], I32, 24 * KIB)
-        nc.sync.dma_start(w4_raw[:], w4_words.rearrange("a p c -> p a c").bitcast(I32))
-        w4s_raw = placed("w4s_raw", [P, KP, H // 4], I32, 116 * KIB)
-        nc.vector.memset(w4s_raw[:], 0)
-        for q in range(4):
-            nc.sync.dma_start(w4s_raw[32 * q : 32 * q + 4, :, :],
-                              w4_scales[:, 4 * q : 4 * q + 4, :].rearrange("a r c -> r a c").bitcast(I32))
-        load_tab(1)
-        load_tab(2)
-        moved = kept("moved", [P, KP - 1, S // 4], I32)
-        nc.vector.memset(moved[:], 0)
-        one = kept("one", [P, 1], F32)
-        nc.vector.memset(one[:], 1.0)
-        minus_one = one
-        warm = kept("warm", [P, 1], F32)
-        nc.scalar.activation(out=warm[:], in_=one[:], func=ACT.Sqrt, bias=one[:])
+        one = tile("one", [P, 1], F32)
+        nc.scalar.activation(out=one[:], in_=unit[:], func=ACT.Sqrt)
+        tab_win = [tile("tab_win%d" % a, [P, T], I32) for a in range(KP)]
+        for a in range(KP):
+            nc.sync.dma_start(tab_win[a][:], tab_words[a].rearrange("p t i -> p (t i)").bitcast(I32))
+            if a == 0:
+                for q in range(4):
+                    nc.sync.dma_start(w4s_raw[32 * q : 32 * q + 4, :, :],
+                                      w4_scales[:, 4 * q : 4 * q + 4, :].rearrange("a r c -> r a c").bitcast(I32))
+        w2_raw = [tile("w2_raw%d" % b, [P, 4, N], F32) for b in range(HP)]
+        w2_rows = w2.rearrange("(b q t i) n -> b t q i n", b=HP, q=16, t=4)
+        for b in range(HP):
+            for t in range(4):
+                nc.sync.dma_start(w2_raw[b][:, t, :], w2_rows[b, t])
+        g_win = [tile("g_win%d" % m, [P, T], F32) for m in range(NT)]
+        for m in range(NT):
+            nc.sync.dma_start(g_win[m][:], gT[P * m : P * (m + 1), :])
 
-        v_tiles = []
-
-        def gather_tab(a, j0, j1, offset):
-            name = "v%d_%d" % (a, j0)
-            tile = kept(name, [P, j1 - j0], U32) if offset is None else placed(name, [P, j1 - j0], U32, offset)
-            v_tiles.append((a, j0, j1, tile))
-            nc.vector.tensor_copy(tile[:], tab_win[a][:].bitcast(U32).indirect(picks(j0, j1)))
-
-        def v_cols(a, j0, j1):
-            for pass_, lo, hi, tile in v_tiles:
-                if pass_ == a and lo <= j0 and j1 <= hi:
-                    return tile[:, j0 - lo : j1 - lo]
-            raise ValueError("no tile")
-
-        gather_tab(0, 0, 512, None)
-        v_scales = kept("v_scales", [P, S], U8)
+        w4_codes = tile("w4_codes", [P, KP, H // 2], I32)
+        for a in range(KP):
+            nc.vector.tensor_copy(w4_codes[:, a, :].rearrange("p (b t q w) -> p b t q w", b=HP, t=4, q=16),
+                                  w4_raw[:, a, :].rearrange("p (b q t w) -> p b t q w", b=HP, t=4, q=16))
+        v_scales = tile("v_scales", [P, S], U8)
         nc.vector.tensor_copy(v_scales[:], scale_win[:].bitcast(U8).indirect(picks(0, S)))
         for a in range(1, KP):
-            (nc.scalar, nc.sync)[a - 1].dma_start(moved[0:MOVE_ROWS, a - 1, :], v_scales[4 * a : 4 * a + MOVE_ROWS, :].bitcast(I32))
+            nc.scalar.dma_start(moved[0:MOVE_ROWS, a - 1, :], v_scales[4 * a : 4 * a + MOVE_ROWS, :].bitcast(I32))
+        w4_planes = tile("w4_planes", [P, KP, H // 4], I32)
+        nc.vector.tensor_copy(w4_planes[:].rearrange("p a (b t q w) -> p (a b) t q w", b=HP, t=4, q=16),
+                              w4s_raw[:].rearrange("p a (b q t w) -> p (a b) t q w", b=HP, t=4, q=16))
 
         def v_plane(a, j0, j1):
             if a == 0:
                 return v_scales[:, j0:j1]
             return moved[:, a - 1, j0 // 4 : j1 // 4].bitcast(U8)
 
-        w4_codes = placed("w4_codes", [P, KP, H // 2], I32, 0)
-        for a in range(KP):
-            nc.vector.tensor_copy(w4_codes[:, a, :].rearrange("p (b t q w) -> p b t q w", b=HP, t=4, q=16),
-                                  w4_raw[:, a, :].rearrange("p (b q t w) -> p b t q w", b=HP, t=4, q=16))
-        gather_tab(1, 0, 512, 24 * KIB + 64)
-        w4_planes = placed("w4_planes", [P, KP, H // 4], I32, 26 * KIB + 64)
-        nc.vector.tensor_copy(w4_planes[:].rearrange("p a (b t q w) -> p (a b) t q w", b=HP, t=4, q=16),
-                              w4s_raw[:].rearrange("p a (b q t w) -> p (a b) t q w", b=HP, t=4, q=16))
-        gather_tab(2, 0, 256, 116 * KIB + 64)
-        gather_tab(2, 256, 512, 117 * KIB + 64)
-        gather_tab(2, 512, 1024, 118 * KIB + 64)
-        gather_tab(1, 512, 1024, 72 * KIB)
-        gather_tab(0, 512, 1024, 70 * KIB)
+        v_tiles = []
 
-        g_win = [placed("g_win%d" % m, [P, T], F32, (29 * KIB + 64, 54 * KIB, 62 * KIB, 46 * KIB)[m]) for m in range(NT)]
+        def gather_tab(a, j0, j1, offset=None):
+            picked = tile("v%d_%d" % (a, j0), [P, j1 - j0], U32, offset)
+            v_tiles.append((a, j0, j1, picked))
+            nc.vector.tensor_copy(picked[:], tab_win[a][:].bitcast(U32).indirect(picks(j0, j1)))
 
-        def load_g(m):
-            nc.sync.dma_start(g_win[m][:], gT[P * m : P * (m + 1), :])
+        def v_cols(a, j0, j1):
+            for pass_, lo, hi, picked in v_tiles:
+                if pass_ == a and lo <= j0 and j1 <= hi:
+                    return picked[:, j0 - lo : j1 - lo]
+            raise ValueError("no tile")
 
-        load_g(0)
-        w2_raw = placed("w2_raw", [P, 4 * HP, N], F32, 100 * KIB + 64)
-        w2_rows = w2.rearrange("(b q t i) n -> b t q i n", b=HP, q=16, t=4)
-        for b in range(HP):
-            for t in range(4):
-                nc.scalar.dma_start(w2_raw[:, 4 * b + t, :], w2_rows[b, t])
-        for m in range(1, NT):
-            load_g(m)
+        def bank_tile(shape, bank):
+            return psum.tile(shape, F32, name="bank", tag="bank%d" % bank)
 
-        h_codes = kept("h_codes", [P, HP, S], U32)
-        h_scales = kept("h_scales", [P, HP, S], U8)
-        turn = [0]
-
-        def decode(b, j0, j1, offset):
-            name = "h%d_%d" % (b, j0)
-            shape = [P, j1 - j0, 4]
-            grouped = kept(name, shape, BF16) if offset is None else placed(name, shape, BF16, offset)
-            for j in range(j0, j1, P):
-                bank = psum.tile([P, 4, P], F32, name="decode_bank", tag="bank%d" % (turn[0] % 4))
-                turn.append(turn.pop() + 1)
+        def decode_passes(bank, b, j, passes):
+            for a in passes:
                 for t in range(4):
-                    for a in range(KP):
-                        nc.tensor.matmul_mx(
-                            out=bank[:, t, :],
-                            lhsT=w4_codes[:, a, 256 * b + 64 * t : 256 * b + 64 * (t + 1)].bitcast(U8).bitcast(FP4X4),
-                            lhsT_scale=w4_planes[:, a, 128 * b + 32 * t : 128 * b + 32 * (t + 1)].bitcast(U8),
-                            rhs=v_cols(a, j, j + P).bitcast(FP8X4),
-                            rhs_scale=v_plane(a, j, j + P),
-                            start=(a == 0),
-                            stop=(a == KP - 1),
-                        )
-                nc.scalar.activation(out=grouped[:, j - j0 : j - j0 + P, :], in_=bank[:].rearrange("p t j -> p j t"), func=ACT.Relu)
-            nc.vector.quantize_mx(out=h_codes[:, b, j0:j1].bitcast(FP8X4), scales=h_scales[:, b, j0:j1],
+                    nc.tensor.matmul_mx(
+                        out=bank[:, t, :],
+                        lhsT=w4_codes[:, a, 256 * b + 64 * t : 256 * b + 64 * (t + 1)].bitcast(U8).bitcast(FP4X4),
+                        lhsT_scale=w4_planes[:, a, 128 * b + 32 * t : 128 * b + 32 * (t + 1)].bitcast(U8),
+                        rhs=v_cols(a, j, j + P).bitcast(FP8X4),
+                        rhs_scale=v_plane(a, j, j + P),
+                        start=(a == 0 and t == 0),
+                        stop=(a == KP - 1 and t == 3),
+                    )
+
+        def relu(grouped, bank, j):
+            nc.scalar.activation(out=grouped[:, j % QUARTER : j % QUARTER + P, :], in_=bank[:].rearrange("p t j -> p j t"), func=ACT.Relu)
+
+        h_scales = tile("h_scales", [P, HP, S], U8)
+
+        def quantize_h(codes, grouped, b, j0):
+            nc.vector.quantize_mx(out=codes.bitcast(FP8X4), scales=h_scales[:, b, j0 : j0 + QUARTER],
                                   in_=grouped[:].rearrange("p j t -> p (j t)"))
 
-        w2_codes = kept("w2_codes", [P, HP, N], U32)
-        w2_scales = kept("w2_scales", [P, HP, N], U8)
+        gather_tab(0, 0, HALF)
+        gather_tab(0, HALF, S, 0)
+        early = [(b, j0 + j) for j0 in (0, QUARTER) for b in range(HP) for j in (0, P)]
+        early_banks = [bank_tile([P, 4, P], i) for i in range(BANKS)]
+        for bank, (b, j) in zip(early_banks, early):
+            decode_passes(bank, b, j, [0])
+        gather_tab(1, 0, HALF)
+        gather_tab(1, HALF, S)
+        gather_tab(2, 0, QUARTER)
+        gather_tab(2, QUARTER, HALF)
+        gather_tab(2, HALF, S)
+        first_codes = [tile("first_codes%d" % b, [P, HALF], U32) for b in range(HP)]
+        for i in range(0, BANKS, 2):
+            b, j0 = early[i]
+            grouped = tile("h%d_%d" % (b, j0), [P, QUARTER, 4], BF16)
+            for k in (i, i + 1):
+                decode_passes(early_banks[k], b, early[k][1], [1, 2])
+                relu(grouped, early_banks[k], early[k][1])
+            quantize_h(first_codes[b][:, j0 : j0 + QUARTER], grouped, b, j0)
 
-        def quantize_w2(b):
-            grouped = placed("w2_grouped%d" % b, [P, N, 4], BF16, (79, 87)[b] * KIB)
-            step = N if CAST[b] == "vector" else P
-            for n0 in range(0, N, step):
-                dst = grouped[:, n0 : n0 + step, :]
-                src = w2_raw[:, 4 * b : 4 * b + 4, n0 : n0 + step].rearrange("p t n -> p n t")
-                if CAST[b] == "vector":
-                    nc.vector.tensor_copy(dst, src)
-                elif CAST[b] == "gpsimd":
-                    nc.gpsimd.tensor_scalar(dst, src, 1.0, 0.0, ALU.mult, ALU.add)
-                else:
-                    nc.scalar.copy(dst, src)
+        w2_codes = tile("w2_codes", [P, HP, N], U32)
+        w2_scales = tile("w2_scales", [P, HP, N], U8)
+        for b in range(HP):
+            grouped = tile("w2_grouped%d" % b, [P, N, 4], BF16)
+            nc.vector.tensor_copy(grouped[:].rearrange("p (c i) t -> p c t i", i=4), w2_raw[b][:].rearrange("p t (c i) -> p c t i", i=4))
             nc.vector.quantize_mx(out=w2_codes[:, b, :].bitcast(FP8X4), scales=w2_scales[:, b, :],
                                   in_=grouped[:].rearrange("p n t -> p (n t)"))
 
-        g_tiles = []
-
-        def gather_g(m, j0, j1, offset):
-            name = "g%d_%d" % (m, j0)
-            tile = kept(name, [P, j1 - j0], F32) if offset is None else placed(name, [P, j1 - j0], F32, offset)
-            g_tiles.append((m, j0, j1, tile))
-            nc.vector.tensor_copy(tile[:], g_win[m][:].indirect(picks(j0, j1)))
-
-        def g_cols(m, j0, j1):
-            for row, lo, hi, tile in g_tiles:
-                if row == m and lo <= j0 and j1 <= hi:
-                    return tile[:, j0 - lo : j1 - lo]
-            raise ValueError("no tile")
-
-        out_rows = out.rearrange("(m p) j -> p m j", p=P)
-        unit = [0]
-
-        def project(m0, m1, j0, j1):
-            u = unit.pop()
-            unit.append(u + 1)
-            bank = psum.tile([P, m1 - m0, j1 - j0], F32, name="project_bank", tag="bank%d" % (4 + u % 4))
-            for m in range(m0, m1):
+        def project(bank_number, rows, j0, codes):
+            width = codes[0].shape[1]
+            bank = bank_tile([P, len(rows), width], bank_number)
+            for i, m in enumerate(rows):
                 for b in range(HP):
                     nc.tensor.matmul_mx(
-                        out=bank[:, m - m0, :],
+                        out=bank[:, i, :],
                         lhsT=w2_codes[:, b, P * m : P * (m + 1)].bitcast(FP8X4),
                         lhsT_scale=w2_scales[:, b, P * m : P * (m + 1)],
-                        rhs=h_codes[:, b, j0:j1].bitcast(FP8X4),
-                        rhs_scale=h_scales[:, b, j0:j1],
+                        rhs=codes[b][:].bitcast(FP8X4),
+                        rhs_scale=h_scales[:, b, j0 : j0 + width],
                         start=(b == 0),
                         stop=(b == HP - 1),
                     )
-            res = kept("res%d" % u, [P, m1 - m0, j1 - j0], F32)
-            for m in range(m0, m1):
-                nc.vector.tensor_tensor(res[:, m - m0, :], bank[:, m - m0, :], g_cols(m, j0, j1), ALU.subtract)
-            nc.scalar.activation(out=res[:], in_=res[:], func=ACT.Square)
-            nc.scalar.activation(out=res[:], in_=res[:], func=ACT.Sqrt, bias=one[:])
-            if MINUS[u] == "vector":
-                nc.vector.tensor_scalar(res[:], res[:], 1.0, -1.0, ALU.mult, ALU.add)
-            elif MINUS[u] == "gpsimd":
-                nc.gpsimd.tensor_scalar(res[:], res[:], 1.0, -1.0, ALU.mult, ALU.add)
-            else:
-                nc.scalar.activation(out=res[:], in_=res[:], func=ACT.Identity, bias=minus_one[:])
-            nc.sync.dma_start(out_rows[:, m0:m1, j0:j1], res[:])
+            return bank
 
-        decode(0, 0, 256, 82 * KIB)
-        decode(1, 0, 256, 90 * KIB)
-        quantize_w2(0)
-        gather_g(0, 0, 512, 78912)
-        decode(0, 256, 512, 126 * KIB)
-        quantize_w2(1)
-        decode(1, 256, 512, 132 * KIB)
-        gather_g(0, 512, 1024, 127040)
-        decode(0, 512, 768, 138 * KIB)
-        project(0, 1, 0, 512)
-        gather_g(1, 0, 512, 133184)
-        decode(1, 512, 768, 144 * KIB)
-        project(1, 2, 0, 512)
-        gather_g(1, 512, 1024, 78912)
-        gather_g(2, 0, 512, 139328)
-        decode(0, 768, 896, 150 * KIB)
-        decode(1, 768, 896, 156 * KIB)
-        project(2, 3, 0, 512)
-        gather_g(2, 512, 1024, 133184)
-        gather_g(3, 0, 512, 145472)
-        project(0, 2, 512, 768)
-        decode(0, 896, 1024, 162 * KIB)
-        decode(1, 896, 1024, None)
-        project(3, 4, 0, 512)
-        gather_g(3, 512, 1024, 139328)
-        project(2, 4, 512, 768)
-        project(0, 4, 768, 896)
-        project(0, 4, 896, 1024)
+        def decode_late(b, j0, banks, offset=None):
+            grouped = tile("h%d_%d" % (b, j0), [P, QUARTER, 4], BF16, offset)
+            for i, j in enumerate((j0, j0 + P)):
+                bank = bank_tile([P, 4, P], banks[i])
+                decode_passes(bank, b, j, range(KP))
+                relu(grouped, bank, j)
+            return grouped
+
+        def gather_g(dst, m, j0, j1):
+            nc.vector.tensor_copy(dst, g_win[m][:].indirect(picks(j0, j1)))
+
+        out_rows = out.rearrange("(m p) j -> p m j", p=P)
+
+        def finish(bank, observed, m0, j0, square, minus, offset=None):
+            rows, width = bank.shape[1], bank.shape[2]
+            res = tile("res%d_%d" % (m0, j0), [P, rows, width], F32, offset)
+            nc.vector.tensor_tensor(res[:], bank[:], observed[:], ALU.subtract)
+            if square == "vector":
+                nc.vector.tensor_tensor(res[:], res[:], res[:], ALU.mult)
+            else:
+                nc.scalar.activation(out=res[:], in_=res[:], func=ACT.Square)
+            nc.scalar.activation(out=res[:], in_=res[:], func=ACT.Sqrt, bias=one[:])
+            minus.tensor_scalar(res[:], res[:], 1.0, -1.0, ALU.mult, ALU.add)
+            nc.sync.dma_start(out_rows[:, m0 : m0 + rows, j0 : j0 + width], res[:])
+
+        MINUS = nc.gpsimd
+        first_banks = [project(2 + m, [m], 0, first_codes) for m in range(NT)]
+        g_first = [tile("g_first%d" % m, [P, 1, HALF], F32, (5, 8, 11, 15)[m] * KIB) for m in range(NT)]
+        g_third = [tile("g_third%d" % i, [P, 2, QUARTER], F32) for i in range(2)]
+        g_fourth = [tile("g_fourth%d" % i, [P, 2, QUARTER], F32) for i in range(2)]
+
+        def gather_late(m):
+            gather_g(g_third[m // 2][:, m % 2, :], m, HALF, HALF + QUARTER)
+            gather_g(g_fourth[m // 2][:, m % 2, :], m, HALF + QUARTER, S)
+
+        third_codes = [tile("third_codes%d" % b, [P, QUARTER], U32, (None, 10 * KIB + 64)[b]) for b in range(HP)]
+        fourth_codes = [tile("fourth_codes%d" % b, [P, QUARTER], U32, (14 + b) * KIB + 64) for b in range(HP)]
+
+        gather_g(g_first[0][:, 0, :], 0, 0, HALF)
+        gather_late(0)
+        finish(first_banks[0], g_first[0], 0, 0, "scalar", MINUS)
+        quantize_h(third_codes[0][:], decode_late(0, HALF, (0, 1)), 0, HALF)
+        third_b1 = decode_late(1, HALF, (7, 0), 5 * KIB)
+
+        gather_g(g_first[1][:, 0, :], 1, 0, HALF)
+        finish(first_banks[1], g_first[1], 1, 0, "scalar", MINUS)
+        gather_late(1)
+        fourth_b0 = decode_late(0, HALF + QUARTER, (1, 7), 8 * KIB)
+
+        gather_g(g_first[2][:, 0, :], 2, 0, HALF)
+        finish(first_banks[2], g_first[2], 2, 0, "scalar", MINUS)
+        quantize_h(third_codes[1][:], third_b1, 1, HALF)
+        third_banks = [project((6, 2)[i], [2 * i, 2 * i + 1], HALF, third_codes) for i in range(2)]
+        gather_late(2)
+        fourth_b1 = decode_late(1, HALF + QUARTER, (0, 1), 11 * KIB + 64)
+
+        gather_g(g_first[3][:, 0, :], 3, 0, HALF)
+        finish(first_banks[3], g_first[3], 3, 0, "scalar", MINUS)
+        quantize_h(fourth_codes[0][:], fourth_b0, 0, HALF + QUARTER)
+        quantize_h(fourth_codes[1][:], fourth_b1, 1, HALF + QUARTER)
+        fourth_banks = [project(3 + i, [2 * i, 2 * i + 1], HALF + QUARTER, fourth_codes) for i in range(2)]
+        finish(third_banks[0], g_third[0], 0, HALF, "scalar", MINUS, 16 * KIB + 64)
+        gather_g(g_third[1][:, 1, :], 3, HALF, HALF + QUARTER)
+        finish(third_banks[1], g_third[1], 2, HALF, "scalar", MINUS)
+        finish(fourth_banks[0], g_fourth[0], 0, HALF + QUARTER, "scalar", nc.vector)
+        gather_g(g_fourth[1][:, 1, :], 3, HALF + QUARTER, S)
+        finish(fourth_banks[1], g_fourth[1], 2, HALF + QUARTER, "vector", nc.vector)

@@ -47,7 +47,7 @@ def tile_list_pseudo_huber_reprojection_kernel(tc, tab_words, tab_scales, offs, 
 
         scale_win = tile("scale_win", [P, T // 4], I32)
         nc.vector.memset(scale_win[:], 0)
-        w4s_raw = tile("w4s_raw", [P, KP, H // 4], I32, 0)
+        w4s_raw = tile("w4s_raw", [P, KP, H // 4], I32)
         nc.vector.memset(w4s_raw[:], 0)
         moved = tile("moved", [P, KP - 1, S // 4], I32)
         nc.vector.memset(moved[:], 0)
@@ -58,16 +58,15 @@ def tile_list_pseudo_huber_reprojection_kernel(tc, tab_words, tab_scales, offs, 
         for q in range(4):
             queue = nc.scalar if q % 2 else nc.sync
             queue.dma_start(scale_win[32 * q : 32 * q + 4 * KP, :], tab_scales[:, 4 * q : 4 * q + 4, :].bitcast(I32))
+        for q in range(4):
+            nc.scalar.dma_start(w4s_raw[32 * q : 32 * q + 4, :, :],
+                                w4_scales[:, 4 * q : 4 * q + 4, :].rearrange("a r c -> r a c").bitcast(I32))
         one = tile("one", [P, 1], F32)
         nc.scalar.activation(out=one[:], in_=unit[:], func=ACT.Sqrt)
         tab_win = [tile("tab_win%d" % a, [P, T], I32) for a in range(KP)]
         for a in range(KP):
             nc.sync.dma_start(tab_win[a][:], tab_words[a].rearrange("p t i -> p (t i)").bitcast(I32))
-            if a == 0:
-                for q in range(4):
-                    nc.sync.dma_start(w4s_raw[32 * q : 32 * q + 4, :, :],
-                                      w4_scales[:, 4 * q : 4 * q + 4, :].rearrange("a r c -> r a c").bitcast(I32))
-        w2_raw = [tile("w2_raw%d" % b, [P, 4, N], F32) for b in range(HP)]
+        w2_raw = [tile("w2_raw%d" % b, [P, 4, N], F32, (0, None)[b]) for b in range(HP)]
         w2_rows = w2.rearrange("(b q t i) n -> b t q i n", b=HP, q=16, t=4)
         for b in range(HP):
             for t in range(4):
@@ -132,32 +131,34 @@ def tile_list_pseudo_huber_reprojection_kernel(tc, tab_words, tab_scales, offs, 
                                   in_=grouped[:].rearrange("p j t -> p (j t)"))
 
         gather_tab(0, 0, HALF)
-        gather_tab(0, HALF, S, 0)
+        gather_tab(0, HALF, S)
         early = [(b, j0 + j) for j0 in (0, QUARTER) for b in range(HP) for j in (0, P)]
         early_banks = [bank_tile([P, 4, P], i) for i in range(BANKS)]
         for bank, (b, j) in zip(early_banks, early):
             decode_passes(bank, b, j, [0])
-        gather_tab(1, 0, HALF)
-        gather_tab(1, HALF, S)
+        gather_tab(1, 0, S)
         gather_tab(2, 0, QUARTER)
         gather_tab(2, QUARTER, HALF)
         gather_tab(2, HALF, S)
+        w2_codes = tile("w2_codes", [P, HP, N], U32)
+        w2_scales = tile("w2_scales", [P, HP, N], U8)
+
+        def quantize_w2(b, cast):
+            grouped = tile("w2_grouped%d" % b, [P, N, 4], BF16)
+            cast(grouped[:].rearrange("p (c i) t -> p c t i", i=4), w2_raw[b][:].rearrange("p t (c i) -> p c t i", i=4))
+            nc.vector.quantize_mx(out=w2_codes[:, b, :].bitcast(FP8X4), scales=w2_scales[:, b, :],
+                                  in_=grouped[:].rearrange("p n t -> p (n t)"))
+
+        quantize_w2(0, nc.scalar.copy)
         first_codes = [tile("first_codes%d" % b, [P, HALF], U32) for b in range(HP)]
         for i in range(0, BANKS, 2):
             b, j0 = early[i]
-            grouped = tile("h%d_%d" % (b, j0), [P, QUARTER, 4], BF16)
+            grouped = tile("h%d_%d" % (b, j0), [P, QUARTER, 4], BF16, KIB * i)
             for k in (i, i + 1):
                 decode_passes(early_banks[k], b, early[k][1], [1, 2])
                 relu(grouped, early_banks[k], early[k][1])
             quantize_h(first_codes[b][:, j0 : j0 + QUARTER], grouped, b, j0)
-
-        w2_codes = tile("w2_codes", [P, HP, N], U32)
-        w2_scales = tile("w2_scales", [P, HP, N], U8)
-        for b in range(HP):
-            grouped = tile("w2_grouped%d" % b, [P, N, 4], BF16)
-            nc.vector.tensor_copy(grouped[:].rearrange("p (c i) t -> p c t i", i=4), w2_raw[b][:].rearrange("p t (c i) -> p c t i", i=4))
-            nc.vector.quantize_mx(out=w2_codes[:, b, :].bitcast(FP8X4), scales=w2_scales[:, b, :],
-                                  in_=grouped[:].rearrange("p n t -> p (n t)"))
+        quantize_w2(1, nc.vector.tensor_copy)
 
         def project(bank_number, rows, j0, codes):
             width = codes[0].shape[1]
@@ -183,62 +184,50 @@ def tile_list_pseudo_huber_reprojection_kernel(tc, tab_words, tab_scales, offs, 
                 relu(grouped, bank, j)
             return grouped
 
-        def gather_g(dst, m, j0, j1):
-            nc.vector.tensor_copy(dst, g_win[m][:].indirect(picks(j0, j1)))
-
         out_rows = out.rearrange("(m p) j -> p m j", p=P)
 
-        def finish(bank, observed, m0, j0, square, minus, offset=None):
-            rows, width = bank.shape[1], bank.shape[2]
-            res = tile("res%d_%d" % (m0, j0), [P, rows, width], F32, offset)
-            nc.vector.tensor_tensor(res[:], bank[:], observed[:], ALU.subtract)
+        def finish(res, m0, j0, square):
+            rows, width = res.shape[1], res.shape[2]
             if square == "vector":
                 nc.vector.tensor_tensor(res[:], res[:], res[:], ALU.mult)
             else:
                 nc.scalar.activation(out=res[:], in_=res[:], func=ACT.Square)
             nc.scalar.activation(out=res[:], in_=res[:], func=ACT.Sqrt, bias=one[:])
-            minus.tensor_scalar(res[:], res[:], 1.0, -1.0, ALU.mult, ALU.add)
+            nc.vector.tensor_scalar(res[:], res[:], 1.0, -1.0, ALU.mult, ALU.add)
             nc.sync.dma_start(out_rows[:, m0 : m0 + rows, j0 : j0 + width], res[:])
 
-        MINUS = nc.gpsimd
-        first_banks = [project(2 + m, [m], 0, first_codes) for m in range(NT)]
-        g_first = [tile("g_first%d" % m, [P, 1, HALF], F32, (5, 8, 11, 15)[m] * KIB) for m in range(NT)]
-        g_third = [tile("g_third%d" % i, [P, 2, QUARTER], F32) for i in range(2)]
-        g_fourth = [tile("g_fourth%d" % i, [P, 2, QUARTER], F32) for i in range(2)]
+        def evacuate(bank, m0, j0):
+            predicted = tile("p%d_%d" % (m0, j0), list(bank.shape), F32)
+            nc.scalar.copy(predicted[:], bank[:])
+            return predicted
 
-        def gather_late(m):
-            gather_g(g_third[m // 2][:, m % 2, :], m, HALF, HALF + QUARTER)
-            gather_g(g_fourth[m // 2][:, m % 2, :], m, HALF + QUARTER, S)
+        def finish_fused(predicted, m0, j0, square):
+            rows, width = predicted.shape[1], predicted.shape[2]
+            res = tile("res%d_%d" % (m0, j0), [P, rows, width], F32)
+            for i in range(rows):
+                nc.vector.tensor_tensor(res[:, i, :], g_win[m0 + i][:].indirect(picks(j0, j0 + width)), predicted[:, i, :], ALU.subtract)
+            finish(res, m0, j0, square)
 
-        third_codes = [tile("third_codes%d" % b, [P, QUARTER], U32, (None, 10 * KIB + 64)[b]) for b in range(HP)]
-        fourth_codes = [tile("fourth_codes%d" % b, [P, QUARTER], U32, (14 + b) * KIB + 64) for b in range(HP)]
+        THIRD, FOURTH = HALF, HALF + QUARTER
+        first = [evacuate(project(2 + m, [m], 0, first_codes), m, 0) for m in range(NT)]
+        third_codes = [tile("third_codes%d" % b, [P, QUARTER], U32) for b in range(HP)]
+        fourth_codes = [tile("fourth_codes%d" % b, [P, QUARTER], U32) for b in range(HP)]
 
-        gather_g(g_first[0][:, 0, :], 0, 0, HALF)
-        gather_late(0)
-        finish(first_banks[0], g_first[0], 0, 0, "scalar", MINUS)
-        quantize_h(third_codes[0][:], decode_late(0, HALF, (0, 1)), 0, HALF)
-        third_b1 = decode_late(1, HALF, (7, 0), 5 * KIB)
-
-        gather_g(g_first[1][:, 0, :], 1, 0, HALF)
-        finish(first_banks[1], g_first[1], 1, 0, "scalar", MINUS)
-        gather_late(1)
-        fourth_b0 = decode_late(0, HALF + QUARTER, (1, 7), 8 * KIB)
-
-        gather_g(g_first[2][:, 0, :], 2, 0, HALF)
-        finish(first_banks[2], g_first[2], 2, 0, "scalar", MINUS)
-        quantize_h(third_codes[1][:], third_b1, 1, HALF)
-        third_banks = [project((6, 2)[i], [2 * i, 2 * i + 1], HALF, third_codes) for i in range(2)]
-        gather_late(2)
-        fourth_b1 = decode_late(1, HALF + QUARTER, (0, 1), 11 * KIB + 64)
-
-        gather_g(g_first[3][:, 0, :], 3, 0, HALF)
-        finish(first_banks[3], g_first[3], 3, 0, "scalar", MINUS)
-        quantize_h(fourth_codes[0][:], fourth_b0, 0, HALF + QUARTER)
-        quantize_h(fourth_codes[1][:], fourth_b1, 1, HALF + QUARTER)
-        fourth_banks = [project(3 + i, [2 * i, 2 * i + 1], HALF + QUARTER, fourth_codes) for i in range(2)]
-        finish(third_banks[0], g_third[0], 0, HALF, "scalar", MINUS, 16 * KIB + 64)
-        gather_g(g_third[1][:, 1, :], 3, HALF, HALF + QUARTER)
-        finish(third_banks[1], g_third[1], 2, HALF, "scalar", MINUS)
-        finish(fourth_banks[0], g_fourth[0], 0, HALF + QUARTER, "scalar", nc.vector)
-        gather_g(g_fourth[1][:, 1, :], 3, HALF + QUARTER, S)
-        finish(fourth_banks[1], g_fourth[1], 2, HALF + QUARTER, "vector", nc.vector)
+        third_b0 = decode_late(0, THIRD, (0, 1))
+        third_b1 = decode_late(1, THIRD, (7, 0))
+        finish_fused(first[0], 0, 0, "scalar")
+        quantize_h(third_codes[0][:], third_b0, 0, THIRD)
+        finish_fused(first[1], 1, 0, "scalar")
+        quantize_h(third_codes[1][:], third_b1, 1, THIRD)
+        third = [evacuate(project((6, 2)[i], [2 * i, 2 * i + 1], THIRD, third_codes), 2 * i, THIRD) for i in range(2)]
+        fourth_b0 = decode_late(0, FOURTH, (1, 7))
+        finish_fused(first[2], 2, 0, "scalar")
+        fourth_b1 = decode_late(1, FOURTH, (0, 1))
+        finish_fused(first[3], 3, 0, "scalar")
+        quantize_h(fourth_codes[0][:], fourth_b0, 0, FOURTH)
+        quantize_h(fourth_codes[1][:], fourth_b1, 1, FOURTH)
+        fourth = [evacuate(project(3 + i, [2 * i, 2 * i + 1], FOURTH, fourth_codes), 2 * i, FOURTH) for i in range(2)]
+        finish_fused(third[0], 0, THIRD, "scalar")
+        finish_fused(third[1], 2, THIRD, "scalar")
+        finish_fused(fourth[0], 0, FOURTH, "scalar")
+        finish_fused(fourth[1], 2, FOURTH, "vector")

@@ -45,65 +45,91 @@ def tile_list_pseudo_huber_reprojection_kernel(tc, tab_words, tab_scales, offs, 
         def picks(j0, j1):
             return offsets[:, j0 // 16 : j1 // 16]
 
-        scale_win = tile("scale_win", [P, T // 4], I32)
+        scale_win = tile("scale_win", [P, T // 4], I32, 16 * KIB)
         nc.vector.memset(scale_win[:], 0)
-        w4s_raw = tile("w4s_raw", [P, KP, H // 4], I32)
+        w4s_raw = tile("w4s_raw", [P, KP, H // 4], I32, 8 * KIB)
         nc.vector.memset(w4s_raw[:], 0)
-        moved = tile("moved", [P, KP - 1, S // 4], I32)
-        nc.vector.memset(moved[:], 0)
+        moved = [tile("moved%d" % i, [P, HALF // 4], I32) for i in range(2 * (KP - 1))]
+        for plane in moved:
+            nc.vector.memset(plane[:], 0)
         unit = tile("unit", [P, 1], F32)
         nc.vector.memset(unit[:], 1.0)
-        w4_raw = tile("w4_raw", [P, KP, H // 2], I32)
-        nc.sync.dma_start(w4_raw[:], w4_words.rearrange("a p c -> p a c").bitcast(I32))
+
+        tab_first = tile("tab_first", [P, T], I32)
+        nc.sync.dma_start(tab_first[:], tab_words[0].rearrange("p t i -> p (t i)").bitcast(I32))
         for q in range(4):
             queue = nc.scalar if q % 2 else nc.sync
             queue.dma_start(scale_win[32 * q : 32 * q + 4 * KP, :], tab_scales[:, 4 * q : 4 * q + 4, :].bitcast(I32))
+
+        def load_w4_scales(queue, q):
+            queue.dma_start(w4s_raw[32 * q : 32 * q + 4, :, :], w4_scales[:, 4 * q : 4 * q + 4, :].rearrange("a r c -> r a c").bitcast(I32))
+
         for q in range(4):
-            nc.scalar.dma_start(w4s_raw[32 * q : 32 * q + 4, :, :],
-                                w4_scales[:, 4 * q : 4 * q + 4, :].rearrange("a r c -> r a c").bitcast(I32))
-        one = tile("one", [P, 1], F32)
-        nc.scalar.activation(out=one[:], in_=unit[:], func=ACT.Sqrt)
-        tab_win = [tile("tab_win%d" % a, [P, T], I32) for a in range(KP)]
-        for a in range(KP):
-            nc.sync.dma_start(tab_win[a][:], tab_words[a].rearrange("p t i -> p (t i)").bitcast(I32))
-        w2_raw = [tile("w2_raw%d" % b, [P, 4, N], F32, (0, None)[b]) for b in range(HP)]
-        w2_rows = w2.rearrange("(b q t i) n -> b t q i n", b=HP, q=16, t=4)
-        for b in range(HP):
-            for t in range(4):
-                nc.sync.dma_start(w2_raw[b][:, t, :], w2_rows[b, t])
-        g_win = [tile("g_win%d" % m, [P, T], F32) for m in range(NT)]
-        for m in range(NT):
-            nc.sync.dma_start(g_win[m][:], gT[P * m : P * (m + 1), :])
-
-        w4_codes = tile("w4_codes", [P, KP, H // 2], I32)
-        for a in range(KP):
-            nc.vector.tensor_copy(w4_codes[:, a, :].rearrange("p (b t q w) -> p b t q w", b=HP, t=4, q=16),
-                                  w4_raw[:, a, :].rearrange("p (b q t w) -> p b t q w", b=HP, t=4, q=16))
-        v_scales = tile("v_scales", [P, S], U8)
-        nc.vector.tensor_copy(v_scales[:], scale_win[:].bitcast(U8).indirect(picks(0, S)))
-        for a in range(1, KP):
-            nc.scalar.dma_start(moved[0:MOVE_ROWS, a - 1, :], v_scales[4 * a : 4 * a + MOVE_ROWS, :].bitcast(I32))
-        w4_planes = tile("w4_planes", [P, KP, H // 4], I32)
-        nc.vector.tensor_copy(w4_planes[:].rearrange("p a (b t q w) -> p (a b) t q w", b=HP, t=4, q=16),
-                              w4s_raw[:].rearrange("p a (b q t w) -> p (a b) t q w", b=HP, t=4, q=16))
-
-        def v_plane(a, j0, j1):
-            if a == 0:
-                return v_scales[:, j0:j1]
-            return moved[:, a - 1, j0 // 4 : j1 // 4].bitcast(U8)
+            load_w4_scales(nc.scalar, q)
+        w4_raw = tile("w4_raw", [P, KP, H // 2], I32)
+        nc.sync.dma_start(w4_raw[:], w4_words.rearrange("a p c -> p a c").bitcast(I32))
+        tab_rest = tile("tab_rest", [P, KP - 1, T], I32)
+        nc.sync.dma_start(tab_rest[:], tab_words[1:].rearrange("a p t i -> p a (t i)").bitcast(I32))
+        tab_win = [tab_first[:], tab_rest[:, 0, :], tab_rest[:, 1, :]]
 
         v_tiles = []
 
         def gather_tab(a, j0, j1, offset=None):
             picked = tile("v%d_%d" % (a, j0), [P, j1 - j0], U32, offset)
             v_tiles.append((a, j0, j1, picked))
-            nc.vector.tensor_copy(picked[:], tab_win[a][:].bitcast(U32).indirect(picks(j0, j1)))
+            nc.vector.tensor_copy(picked[:], tab_win[a].bitcast(U32).indirect(picks(j0, j1)))
 
         def v_cols(a, j0, j1):
             for pass_, lo, hi, picked in v_tiles:
                 if pass_ == a and lo <= j0 and j1 <= hi:
                     return picked[:, j0 - lo : j1 - lo]
             raise ValueError("no tile")
+
+        v_scales = [tile("v_scales%d" % half, [P, HALF], U8, (None, 8 * KIB + 64)[half]) for half in range(2)]
+
+        def gather_scales(half):
+            nc.vector.tensor_copy(v_scales[half][:], scale_win[:].bitcast(U8).indirect(picks(HALF * half, HALF * (half + 1))))
+            for a in range(1, KP):
+                nc.scalar.dma_start(moved[2 * half + a - 1][0:MOVE_ROWS, :], v_scales[half][4 * a : 4 * a + MOVE_ROWS, :].bitcast(I32))
+
+        def v_plane(a, j0, j1):
+            half, lo = divmod(j0, HALF)
+            if a == 0:
+                return v_scales[half][:, lo : lo + j1 - j0]
+            return moved[2 * half + a - 1][:, lo // 4 : (lo + j1 - j0) // 4].bitcast(U8)
+
+        gather_tab(0, 0, HALF)
+        gather_scales(0)
+        w4_codes = [tile("w4_codes%d" % a, [P, H // 2], I32, (None, 6 * KIB + 64, 11 * KIB - 64)[a]) for a in range(KP)]
+
+        def deal_w4(a):
+            nc.vector.tensor_copy(w4_codes[a][:].rearrange("p (b t q w) -> p b t q w", b=HP, t=4, q=16),
+                                  w4_raw[:, a, :].rearrange("p (b q t w) -> p b t q w", b=HP, t=4, q=16))
+
+        deal_w4(0)
+        w4_planes = tile("w4_planes", [P, KP, H // 4], I32)
+        nc.vector.tensor_copy(w4_planes[:].rearrange("p a (b t q w) -> p (a b) t q w", b=HP, t=4, q=16),
+                              w4s_raw[:].rearrange("p a (b q t w) -> p (a b) t q w", b=HP, t=4, q=16))
+        one = tile("one", [P, 1], F32, 8 * KIB + 2624)
+        nc.scalar.activation(out=one[:], in_=unit[:], func=ACT.Sqrt)
+        deal_w4(1)
+        deal_w4(2)
+        gather_scales(1)
+        gather_tab(0, HALF, S, 8 * KIB + 576)
+
+        g_win = [tile("g_win%d" % m, [P, T], F32, (16 * KIB, None, None, None)[m]) for m in range(NT)]
+
+        def load_g(m):
+            nc.sync.dma_start(g_win[m][:], gT[P * m : P * (m + 1), :])
+
+        load_g(0)
+        w2_raw = [tile("w2_raw%d" % b, [P, 4, N], F32) for b in range(HP)]
+        w2_rows = w2.rearrange("(b q t i) n -> b t q i n", b=HP, q=16, t=4)
+        for b in range(HP):
+            for t in range(4):
+                nc.sync.dma_start(w2_raw[b][:, t, :], w2_rows[b, t])
+        for m in range(1, NT):
+            load_g(m)
 
         def bank_tile(shape, bank):
             return psum.tile(shape, F32, name="bank", tag="bank%d" % bank)
@@ -113,7 +139,7 @@ def tile_list_pseudo_huber_reprojection_kernel(tc, tab_words, tab_scales, offs, 
                 for t in range(4):
                     nc.tensor.matmul_mx(
                         out=bank[:, t, :],
-                        lhsT=w4_codes[:, a, 256 * b + 64 * t : 256 * b + 64 * (t + 1)].bitcast(U8).bitcast(FP4X4),
+                        lhsT=w4_codes[a][:, 256 * b + 64 * t : 256 * b + 64 * (t + 1)].bitcast(U8).bitcast(FP4X4),
                         lhsT_scale=w4_planes[:, a, 128 * b + 32 * t : 128 * b + 32 * (t + 1)].bitcast(U8),
                         rhs=v_cols(a, j, j + P).bitcast(FP8X4),
                         rhs_scale=v_plane(a, j, j + P),
@@ -130,35 +156,37 @@ def tile_list_pseudo_huber_reprojection_kernel(tc, tab_words, tab_scales, offs, 
             nc.vector.quantize_mx(out=codes.bitcast(FP8X4), scales=h_scales[:, b, j0 : j0 + QUARTER],
                                   in_=grouped[:].rearrange("p j t -> p (j t)"))
 
-        gather_tab(0, 0, HALF)
-        gather_tab(0, HALF, S)
         early = [(b, j0 + j) for j0 in (0, QUARTER) for b in range(HP) for j in (0, P)]
         early_banks = [bank_tile([P, 4, P], i) for i in range(BANKS)]
         for bank, (b, j) in zip(early_banks, early):
             decode_passes(bank, b, j, [0])
-        gather_tab(1, 0, S)
-        gather_tab(2, 0, QUARTER)
-        gather_tab(2, QUARTER, HALF)
-        gather_tab(2, HALF, S)
+        for j0, j1 in ((0, QUARTER), (QUARTER, HALF), (HALF, S)):
+            for a in range(1, KP):
+                gather_tab(a, j0, j1)
         w2_codes = tile("w2_codes", [P, HP, N], U32)
         w2_scales = tile("w2_scales", [P, HP, N], U8)
 
-        def quantize_w2(b, cast):
+        def quantize_w2(b):
             grouped = tile("w2_grouped%d" % b, [P, N, 4], BF16)
-            cast(grouped[:].rearrange("p (c i) t -> p c t i", i=4), w2_raw[b][:].rearrange("p t (c i) -> p c t i", i=4))
+            if b == 0:
+                for n0 in range(0, N, N // 2):
+                    nc.gpsimd.tensor_scalar(grouped[:, n0 : n0 + N // 2, :], w2_raw[b][:, :, n0 : n0 + N // 2].rearrange("p t n -> p n t"),
+                                            1.0, 0.0, ALU.mult, ALU.add)
+            else:
+                nc.vector.tensor_copy(grouped[:].rearrange("p (c i) t -> p c t i", i=4), w2_raw[b][:].rearrange("p t (c i) -> p c t i", i=4))
             nc.vector.quantize_mx(out=w2_codes[:, b, :].bitcast(FP8X4), scales=w2_scales[:, b, :],
                                   in_=grouped[:].rearrange("p n t -> p (n t)"))
 
-        quantize_w2(0, nc.scalar.copy)
         first_codes = [tile("first_codes%d" % b, [P, HALF], U32) for b in range(HP)]
         for i in range(0, BANKS, 2):
             b, j0 = early[i]
-            grouped = tile("h%d_%d" % (b, j0), [P, QUARTER, 4], BF16, KIB * i)
+            grouped = tile("h%d_%d" % (b, j0), [P, QUARTER, 4], BF16)
             for k in (i, i + 1):
                 decode_passes(early_banks[k], b, early[k][1], [1, 2])
                 relu(grouped, early_banks[k], early[k][1])
             quantize_h(first_codes[b][:, j0 : j0 + QUARTER], grouped, b, j0)
-        quantize_w2(1, nc.vector.tensor_copy)
+        quantize_w2(1)
+        quantize_w2(0)
 
         def project(bank_number, rows, j0, codes):
             width = codes[0].shape[1]
@@ -186,48 +214,65 @@ def tile_list_pseudo_huber_reprojection_kernel(tc, tab_words, tab_scales, offs, 
 
         out_rows = out.rearrange("(m p) j -> p m j", p=P)
 
-        def finish(res, m0, j0, square):
+        def finish(res, m0, j0, last):
             rows, width = res.shape[1], res.shape[2]
-            if square == "vector":
+            if last:
                 nc.vector.tensor_tensor(res[:], res[:], res[:], ALU.mult)
             else:
                 nc.scalar.activation(out=res[:], in_=res[:], func=ACT.Square)
             nc.scalar.activation(out=res[:], in_=res[:], func=ACT.Sqrt, bias=one[:])
-            nc.vector.tensor_scalar(res[:], res[:], 1.0, -1.0, ALU.mult, ALU.add)
+            (nc.vector if last else nc.gpsimd).tensor_scalar(res[:], res[:], 1.0, -1.0, ALU.mult, ALU.add)
             nc.sync.dma_start(out_rows[:, m0 : m0 + rows, j0 : j0 + width], res[:])
 
-        def evacuate(bank, m0, j0):
-            predicted = tile("p%d_%d" % (m0, j0), list(bank.shape), F32)
-            nc.scalar.copy(predicted[:], bank[:])
+        def evacuate(bank, m, offset=None):
+            predicted = tile("p%d" % m, [P, HALF], F32, offset)
+            nc.scalar.copy(predicted[:], bank[:, 0, :])
             return predicted
 
-        def finish_fused(predicted, m0, j0, square):
-            rows, width = predicted.shape[1], predicted.shape[2]
-            res = tile("res%d_%d" % (m0, j0), [P, rows, width], F32)
-            for i in range(rows):
-                nc.vector.tensor_tensor(res[:, i, :], g_win[m0 + i][:].indirect(picks(j0, j0 + width)), predicted[:, i, :], ALU.subtract)
-            finish(res, m0, j0, square)
+        def finish_fused(m):
+            res = tile("res%d" % m, [P, 1, HALF], F32)
+            nc.vector.tensor_tensor(res[:, 0, :], g_win[m][:].indirect(picks(0, HALF)), first[m][:], ALU.subtract)
+            finish(res, m, 0, False)
+
+        def finish_gathered(bank, observed, m0, j0, last, offset=None):
+            res = tile("res%d_%d" % (m0, j0), list(bank.shape), F32, offset)
+            nc.vector.tensor_tensor(res[:], bank[:], observed, ALU.subtract)
+            finish(res, m0, j0, last)
 
         THIRD, FOURTH = HALF, HALF + QUARTER
-        first = [evacuate(project(2 + m, [m], 0, first_codes), m, 0) for m in range(NT)]
-        third_codes = [tile("third_codes%d" % b, [P, QUARTER], U32) for b in range(HP)]
-        fourth_codes = [tile("fourth_codes%d" % b, [P, QUARTER], U32) for b in range(HP)]
+        g_first = tile("g_first", [P, 1, HALF], F32)
+        g_late = [tile("g_late%d" % i, [P, 2, HALF], F32) for i in range(2)]
 
+        def gather_late(m):
+            nc.vector.tensor_copy(g_late[m // 2][:, m % 2, :], g_win[m][:].indirect(picks(HALF, S)))
+
+        nc.vector.tensor_copy(g_first[:, 0, :], g_win[0][:].indirect(picks(0, HALF)))
+        gather_late(0)
+        first_banks = [project(2 + m, [m], 0, first_codes) for m in range(NT)]
+        first = {1: evacuate(first_banks[1], 1)}
+        third_codes = [tile("third_codes%d" % b, [P, QUARTER], U32, (None, 26 * KIB)[b]) for b in range(HP)]
+        fourth_codes = [tile("fourth_codes%d" % b, [P, QUARTER], U32, (3 * KIB + 128, 2 * KIB + 128)[b]) for b in range(HP)]
+
+        finish_gathered(first_banks[0], g_first[:], 0, 0, False)
+        first[2] = evacuate(first_banks[2], 2, 26 * KIB)
+        first[3] = evacuate(first_banks[3], 3, 2 * KIB)
         third_b0 = decode_late(0, THIRD, (0, 1))
-        third_b1 = decode_late(1, THIRD, (7, 0))
-        finish_fused(first[0], 0, 0, "scalar")
+        third_b1 = decode_late(1, THIRD, (6, 3))
+        finish_fused(1)
         quantize_h(third_codes[0][:], third_b0, 0, THIRD)
-        finish_fused(first[1], 1, 0, "scalar")
+        gather_late(1)
+        fourth_b0 = decode_late(0, FOURTH, (2, 4))
+        finish_fused(2)
         quantize_h(third_codes[1][:], third_b1, 1, THIRD)
-        third = [evacuate(project((6, 2)[i], [2 * i, 2 * i + 1], THIRD, third_codes), 2 * i, THIRD) for i in range(2)]
-        fourth_b0 = decode_late(0, FOURTH, (1, 7))
-        finish_fused(first[2], 2, 0, "scalar")
-        fourth_b1 = decode_late(1, FOURTH, (0, 1))
-        finish_fused(first[3], 3, 0, "scalar")
+        third = [project(i, [2 * i, 2 * i + 1], THIRD, third_codes) for i in range(2)]
+        gather_late(2)
+        fourth_b1 = decode_late(1, FOURTH, (5, 3))
+        finish_fused(3)
+        gather_late(3)
+        finish_gathered(third[0], g_late[0][:, :, :QUARTER], 0, THIRD, False, 64)
         quantize_h(fourth_codes[0][:], fourth_b0, 0, FOURTH)
         quantize_h(fourth_codes[1][:], fourth_b1, 1, FOURTH)
-        fourth = [evacuate(project(3 + i, [2 * i, 2 * i + 1], FOURTH, fourth_codes), 2 * i, FOURTH) for i in range(2)]
-        finish_fused(third[0], 0, THIRD, "scalar")
-        finish_fused(third[1], 2, THIRD, "scalar")
-        finish_fused(fourth[0], 0, FOURTH, "scalar")
-        finish_fused(fourth[1], 2, FOURTH, "vector")
+        fourth = [project(6 + i, [2 * i, 2 * i + 1], FOURTH, fourth_codes) for i in range(2)]
+        finish_gathered(third[1], g_late[1][:, :, :QUARTER], 2, THIRD, False)
+        for i in range(2):
+            finish_gathered(fourth[i], g_late[i][:, :, QUARTER:], 2 * i, FOURTH, True)

@@ -117,18 +117,17 @@ def tile_list_pseudo_huber_reprojection_kernel(tc, tab_words, tab_scales, offs, 
         gather_scales(1)
         gather_tab(0, HALF, S, 8 * KIB + 576)
 
-        g_win = [tile("g_win%d" % m, [P, T], F32, (16 * KIB, None, None, None)[m]) for m in range(NT)]
+        g_win = [tile("g_win%d" % m, [P, T], F32) for m in range(NT)]
 
         def load_g(m):
             nc.sync.dma_start(g_win[m][:], gT[P * m : P * (m + 1), :])
 
-        load_g(0)
         w2_raw = [tile("w2_raw%d" % b, [P, 4, N], F32) for b in range(HP)]
         w2_rows = w2.rearrange("(b q t i) n -> b t q i n", b=HP, q=16, t=4)
         for b in range(HP):
             for t in range(4):
                 nc.sync.dma_start(w2_raw[b][:, t, :], w2_rows[b, t])
-        for m in range(1, NT):
+        for m in range(NT):
             load_g(m)
 
         def bank_tile(shape, bank):
@@ -166,14 +165,9 @@ def tile_list_pseudo_huber_reprojection_kernel(tc, tab_words, tab_scales, offs, 
         w2_codes = tile("w2_codes", [P, HP, N], U32)
         w2_scales = tile("w2_scales", [P, HP, N], U8)
 
-        def quantize_w2(b):
+        def quantize_w2(b, copy):
             grouped = tile("w2_grouped%d" % b, [P, N, 4], BF16)
-            if b == 0:
-                for n0 in range(0, N, N // 2):
-                    nc.gpsimd.tensor_scalar(grouped[:, n0 : n0 + N // 2, :], w2_raw[b][:, :, n0 : n0 + N // 2].rearrange("p t n -> p n t"),
-                                            1.0, 0.0, ALU.mult, ALU.add)
-            else:
-                nc.vector.tensor_copy(grouped[:].rearrange("p (c i) t -> p c t i", i=4), w2_raw[b][:].rearrange("p t (c i) -> p c t i", i=4))
+            copy(grouped[:].rearrange("p (c i) t -> p c t i", i=4), w2_raw[b][:].rearrange("p t (c i) -> p c t i", i=4))
             nc.vector.quantize_mx(out=w2_codes[:, b, :].bitcast(FP8X4), scales=w2_scales[:, b, :],
                                   in_=grouped[:].rearrange("p n t -> p (n t)"))
 
@@ -185,8 +179,8 @@ def tile_list_pseudo_huber_reprojection_kernel(tc, tab_words, tab_scales, offs, 
                 decode_passes(early_banks[k], b, early[k][1], [1, 2])
                 relu(grouped, early_banks[k], early[k][1])
             quantize_h(first_codes[b][:, j0 : j0 + QUARTER], grouped, b, j0)
-        quantize_w2(1)
-        quantize_w2(0)
+        quantize_w2(0, nc.vector.tensor_copy)
+        quantize_w2(1, nc.scalar.copy)
 
         def project(bank_number, rows, j0, codes):
             width = codes[0].shape[1]
@@ -246,33 +240,28 @@ def tile_list_pseudo_huber_reprojection_kernel(tc, tab_words, tab_scales, offs, 
         def gather_late(m):
             nc.vector.tensor_copy(g_late[m // 2][:, m % 2, :], g_win[m][:].indirect(picks(HALF, S)))
 
+        third_codes = [tile("third_codes%d" % b, [P, QUARTER], U32) for b in range(HP)]
+        fourth_codes = [tile("fourth_codes%d" % b, [P, QUARTER], U32) for b in range(HP)]
         nc.vector.tensor_copy(g_first[:, 0, :], g_win[0][:].indirect(picks(0, HALF)))
         gather_late(0)
-        first_banks = [project(2 + m, [m], 0, first_codes) for m in range(NT)]
-        first = {1: evacuate(first_banks[1], 1)}
-        third_codes = [tile("third_codes%d" % b, [P, QUARTER], U32, (None, 26 * KIB)[b]) for b in range(HP)]
-        fourth_codes = [tile("fourth_codes%d" % b, [P, QUARTER], U32, (3 * KIB + 128, 2 * KIB + 128)[b]) for b in range(HP)]
-
-        finish_gathered(first_banks[0], g_first[:], 0, 0, False)
-        first[2] = evacuate(first_banks[2], 2, 26 * KIB)
-        first[3] = evacuate(first_banks[3], 3, 2 * KIB)
-        third_b0 = decode_late(0, THIRD, (0, 1))
-        third_b1 = decode_late(1, THIRD, (6, 3))
-        finish_fused(1)
-        quantize_h(third_codes[0][:], third_b0, 0, THIRD)
-        gather_late(1)
-        fourth_b0 = decode_late(0, FOURTH, (2, 4))
-        finish_fused(2)
-        quantize_h(third_codes[1][:], third_b1, 1, THIRD)
+        third_h = [decode_late(b, THIRD, (2 * b, 2 * b + 1)) for b in range(HP)]
+        first_banks = [project(4 + m, [m], 0, first_codes) for m in range(NT)]
+        first = {m: evacuate(first_banks[m], m) for m in range(1, NT)}
+        for b in range(HP):
+            quantize_h(third_codes[b][:], third_h[b], b, THIRD)
         third = [project(i, [2 * i, 2 * i + 1], THIRD, third_codes) for i in range(2)]
+        finish_gathered(first_banks[0], g_first[:], 0, 0, False)
+        gather_late(1)
+        fourth_h = [decode_late(0, FOURTH, (5, 6)), decode_late(1, FOURTH, (7, 4), 41 * KIB)]
+        finish_fused(1)
+        finish_gathered(third[0], g_late[0][:, :, :QUARTER], 0, THIRD, False)
         gather_late(2)
-        fourth_b1 = decode_late(1, FOURTH, (5, 3))
+        finish_fused(2)
+        quantize_h(fourth_codes[0][:], fourth_h[0], 0, FOURTH)
         finish_fused(3)
         gather_late(3)
-        finish_gathered(third[0], g_late[0][:, :, :QUARTER], 0, THIRD, False, 64)
-        quantize_h(fourth_codes[0][:], fourth_b0, 0, FOURTH)
-        quantize_h(fourth_codes[1][:], fourth_b1, 1, FOURTH)
-        fourth = [project(6 + i, [2 * i, 2 * i + 1], FOURTH, fourth_codes) for i in range(2)]
-        finish_gathered(third[1], g_late[1][:, :, :QUARTER], 2, THIRD, False)
+        quantize_h(fourth_codes[1][:], fourth_h[1], 1, FOURTH)
+        fourth = [project(2 + i, [2 * i, 2 * i + 1], FOURTH, fourth_codes) for i in range(2)]
+        finish_gathered(third[1], g_late[1][:, :, :QUARTER], 2, THIRD, False, 42 * KIB)
         for i in range(2):
             finish_gathered(fourth[i], g_late[i][:, :, QUARTER:], 2 * i, FOURTH, True)

@@ -58,7 +58,7 @@ def tile_list_pseudo_huber_reprojection_kernel(tc, tab_words, tab_scales, offs, 
         tab_first = tile("tab_first", [P, T], I32)
         nc.sync.dma_start(tab_first[:], tab_words[0].rearrange("p t i -> p (t i)").bitcast(I32))
         for q in range(4):
-            queue = nc.scalar if q % 2 else nc.sync
+            queue = nc.scalar if q else nc.sync
             queue.dma_start(scale_win[32 * q : 32 * q + 4 * KP, :], tab_scales[:, 4 * q : 4 * q + 4, :].bitcast(I32))
 
         def load_w4_scales(queue, q):
@@ -66,7 +66,7 @@ def tile_list_pseudo_huber_reprojection_kernel(tc, tab_words, tab_scales, offs, 
 
         for q in range(4):
             load_w4_scales(nc.scalar, q)
-        w4_raw = tile("w4_raw", [P, KP, H // 2], I32)
+        w4_raw = tile("w4_raw", [P, KP, H // 2], I32, 56 * KIB)
         nc.sync.dma_start(w4_raw[:], w4_words.rearrange("a p c -> p a c").bitcast(I32))
         tab_rest = tile("tab_rest", [P, KP - 1, T], I32)
         nc.sync.dma_start(tab_rest[:], tab_words[1:].rearrange("a p t i -> p a (t i)").bitcast(I32))
@@ -122,7 +122,7 @@ def tile_list_pseudo_huber_reprojection_kernel(tc, tab_words, tab_scales, offs, 
         def load_g(m):
             nc.sync.dma_start(g_win[m][:], gT[P * m : P * (m + 1), :])
 
-        w2_raw = [tile("w2_raw%d" % b, [P, 4, N], F32) for b in range(HP)]
+        w2_raw = [tile("w2_raw%d" % b, [P, 4, N], F32, (56 * KIB, None)[b]) for b in range(HP)]
         w2_rows = w2.rearrange("(b q t i) n -> b t q i n", b=HP, q=16, t=4)
         for b in range(HP):
             for t in range(4):
@@ -147,12 +147,12 @@ def tile_list_pseudo_huber_reprojection_kernel(tc, tab_words, tab_scales, offs, 
                     )
 
         def relu(grouped, bank, j):
-            nc.scalar.activation(out=grouped[:, j % QUARTER : j % QUARTER + P, :], in_=bank[:].rearrange("p t j -> p j t"), func=ACT.Relu)
+            nc.scalar.activation(out=grouped[:, j % grouped.shape[1] : j % grouped.shape[1] + P, :], in_=bank[:].rearrange("p t j -> p j t"), func=ACT.Relu)
 
         h_scales = tile("h_scales", [P, HP, S], U8)
 
         def quantize_h(codes, grouped, b, j0):
-            nc.vector.quantize_mx(out=codes.bitcast(FP8X4), scales=h_scales[:, b, j0 : j0 + QUARTER],
+            nc.vector.quantize_mx(out=codes.bitcast(FP8X4), scales=h_scales[:, b, j0 : j0 + grouped.shape[1]],
                                   in_=grouped[:].rearrange("p j t -> p (j t)"))
 
         early = [(b, j0 + j) for j0 in (0, QUARTER) for b in range(HP) for j in (0, P)]
@@ -172,13 +172,15 @@ def tile_list_pseudo_huber_reprojection_kernel(tc, tab_words, tab_scales, offs, 
                                   in_=grouped[:].rearrange("p n t -> p (n t)"))
 
         first_codes = [tile("first_codes%d" % b, [P, HALF], U32) for b in range(HP)]
-        for i in range(0, BANKS, 2):
-            b, j0 = early[i]
-            grouped = tile("h%d_%d" % (b, j0), [P, QUARTER, 4], BF16)
-            for k in (i, i + 1):
-                decode_passes(early_banks[k], b, early[k][1], [1, 2])
-                relu(grouped, early_banks[k], early[k][1])
-            quantize_h(first_codes[b][:, j0 : j0 + QUARTER], grouped, b, j0)
+        first_h = [tile("first_h%d" % b, [P, HALF, 4], BF16) for b in range(HP)]
+        for i, (bank, (b, j)) in enumerate(zip(early_banks, early)):
+            if i == 0:
+                decode_passes(bank, b, j, [1])
+                decode_passes(early_banks[1], early[1][0], early[1][1], [1])
+            decode_passes(bank, b, j, [2] if i < 2 else [1, 2])
+            relu(first_h[b], bank, j)
+        for b in range(HP):
+            quantize_h(first_codes[b][:], first_h[b], b, 0)
         quantize_w2(0, nc.vector.tensor_copy)
         quantize_w2(1, nc.scalar.copy)
 
@@ -198,6 +200,18 @@ def tile_list_pseudo_huber_reprojection_kernel(tc, tab_words, tab_scales, offs, 
                     )
             return bank
 
+        def project_half(bank, rows, j0, codes, b):
+            for i, m in enumerate(rows):
+                nc.tensor.matmul_mx(
+                    out=bank[:, i, :],
+                    lhsT=w2_codes[:, b, P * m : P * (m + 1)].bitcast(FP8X4),
+                    lhsT_scale=w2_scales[:, b, P * m : P * (m + 1)],
+                    rhs=codes[b][:].bitcast(FP8X4),
+                    rhs_scale=h_scales[:, b, j0 : j0 + QUARTER],
+                    start=(b == 0 and i == 0),
+                    stop=(b == HP - 1 and i == len(rows) - 1),
+                )
+
         def decode_late(b, j0, banks, offset=None):
             grouped = tile("h%d_%d" % (b, j0), [P, QUARTER, 4], BF16, offset)
             for i, j in enumerate((j0, j0 + P)):
@@ -210,7 +224,7 @@ def tile_list_pseudo_huber_reprojection_kernel(tc, tab_words, tab_scales, offs, 
 
         def finish(res, m0, j0, last):
             rows, width = res.shape[1], res.shape[2]
-            if last:
+            if last and m0:
                 nc.vector.tensor_tensor(res[:], res[:], res[:], ALU.mult)
             else:
                 nc.scalar.activation(out=res[:], in_=res[:], func=ACT.Square)
@@ -234,34 +248,41 @@ def tile_list_pseudo_huber_reprojection_kernel(tc, tab_words, tab_scales, offs, 
             finish(res, m0, j0, last)
 
         THIRD, FOURTH = HALF, HALF + QUARTER
-        g_first = tile("g_first", [P, 1, HALF], F32)
-        g_late = [tile("g_late%d" % i, [P, 2, HALF], F32) for i in range(2)]
+        g_low = tile("g_low", [P, 2, HALF], F32)
+        g_third = tile("g_third", [P, 2, QUARTER], F32)
+        g_fourth = tile("g_fourth", [P, 2, QUARTER], F32, 42 * KIB)
 
-        def gather_late(m):
-            nc.vector.tensor_copy(g_late[m // 2][:, m % 2, :], g_win[m][:].indirect(picks(HALF, S)))
+        def gather_g(picked, m, j0):
+            nc.vector.tensor_copy(picked, g_win[m][:].indirect(picks(j0, j0 + picked.shape[1])))
 
         third_codes = [tile("third_codes%d" % b, [P, QUARTER], U32) for b in range(HP)]
         fourth_codes = [tile("fourth_codes%d" % b, [P, QUARTER], U32) for b in range(HP)]
-        nc.vector.tensor_copy(g_first[:, 0, :], g_win[0][:].indirect(picks(0, HALF)))
-        gather_late(0)
+        gather_g(g_low[:, 0, :], 0, HALF)
         third_h = [decode_late(b, THIRD, (2 * b, 2 * b + 1)) for b in range(HP)]
         first_banks = [project(4 + m, [m], 0, first_codes) for m in range(NT)]
-        first = {m: evacuate(first_banks[m], m) for m in range(1, NT)}
+        first = {m: evacuate(first_banks[m], m) for m in range(NT)}
         for b in range(HP):
             quantize_h(third_codes[b][:], third_h[b], b, THIRD)
-        third = [project(i, [2 * i, 2 * i + 1], THIRD, third_codes) for i in range(2)]
-        finish_gathered(first_banks[0], g_first[:], 0, 0, False)
-        gather_late(1)
-        fourth_h = [decode_late(0, FOURTH, (5, 6)), decode_late(1, FOURTH, (7, 4), 41 * KIB)]
+        third_low = project(0, [0, 1], THIRD, third_codes)
+        gather_g(g_low[:, 1, :], 1, HALF)
+        finish_fused(0)
+        fourth_h = [decode_late(0, FOURTH, (4, 5)), decode_late(1, FOURTH, (6, 7), 41 * KIB)]
         finish_fused(1)
-        finish_gathered(third[0], g_late[0][:, :, :QUARTER], 0, THIRD, False)
-        gather_late(2)
+        finish_gathered(third_low, g_low[:, :, :QUARTER], 0, THIRD, False)
+        gather_g(g_third[:, 0, :], 2, THIRD)
         finish_fused(2)
         quantize_h(fourth_codes[0][:], fourth_h[0], 0, FOURTH)
-        finish_fused(3)
-        gather_late(3)
-        quantize_h(fourth_codes[1][:], fourth_h[1], 1, FOURTH)
-        fourth = [project(2 + i, [2 * i, 2 * i + 1], FOURTH, fourth_codes) for i in range(2)]
-        finish_gathered(third[1], g_late[1][:, :, :QUARTER], 2, THIRD, False, 42 * KIB)
+        third_high = project(6, [2, 3], THIRD, third_codes)
+        fourth = [bank_tile([P, 2, QUARTER], 2 + i) for i in range(2)]
         for i in range(2):
-            finish_gathered(fourth[i], g_late[i][:, :, QUARTER:], 2 * i, FOURTH, True)
+            project_half(fourth[i], [2 * i, 2 * i + 1], FOURTH, fourth_codes, 0)
+        gather_g(g_third[:, 1, :], 3, THIRD)
+        finish_fused(3)
+        quantize_h(fourth_codes[1][:], fourth_h[1], 1, FOURTH)
+        for i in range(2):
+            project_half(fourth[i], [2 * i, 2 * i + 1], FOURTH, fourth_codes, 1)
+        finish_gathered(third_high, g_third[:], 2, THIRD, False, 44 * KIB)
+        gather_g(g_fourth[:, 0, :], 2, FOURTH)
+        finish_gathered(fourth[0], g_low[:, :, QUARTER:], 0, FOURTH, True)
+        gather_g(g_fourth[:, 1, :], 3, FOURTH)
+        finish_gathered(fourth[1], g_fourth[:], 2, FOURTH, True)

@@ -23,8 +23,8 @@ NT = N // P
 MOVE_ROWS = 112
 HALF = S // 2
 QUARTER = S // 4
+THIRD, FOURTH = HALF, HALF + QUARTER
 KIB = 1024
-BANKS = 8
 
 
 def tile_list_pseudo_huber_reprojection_kernel(tc, tab_words, tab_scales, offs, w4_words, w4_scales, w2, gT, out):
@@ -39,45 +39,54 @@ def tile_list_pseudo_huber_reprojection_kernel(tc, tab_words, tab_scales, offs, 
                 return held.tile(shape, dtype, name=name, align_bytes=64)
             return shared.tile(shape, dtype, name=name, offset=offset, align_bytes=64)
 
+        SCALE_WIN, COPY_OF_P, LAST_H, W4_SCALES, COPY_OF_LAST_P, W4_FIRST, W2_RAW = 0, 2 * KIB, 4 * KIB, 6 * KIB, 10 * KIB, 12 * KIB, 14 * KIB
+
         offsets = held.tile([P, S // 16], U16, name="offsets")
         nc.sync.dma_start(offsets[:], offs)
 
         def picks(j0, j1):
             return offsets[:, j0 // 16 : j1 // 16]
 
-        scale_win = tile("scale_win", [P, T // 4], I32, 16 * KIB)
-        nc.vector.memset(scale_win[:], 0)
-        w4s_raw = tile("w4s_raw", [P, KP, H // 4], I32, 8 * KIB)
+        scale_win = tile("scale_win", [P, T // 4], I32, SCALE_WIN)
+        nc.gpsimd.memset(scale_win[:], 0)
+        w4s_raw = tile("w4s_raw", [P, KP, H // 4], I32, W4_SCALES)
         nc.vector.memset(w4s_raw[:], 0)
-        moved = [tile("moved%d" % i, [P, HALF // 4], I32) for i in range(2 * (KP - 1))]
+        moves = [(1, 0, HALF), (2, 0, S), (1, HALF, S)]
+        moved = [tile("moved%d" % i, [P, (j1 - j0) // 4], I32) for i, (a, j0, j1) in enumerate(moves)]
         for plane in moved:
             nc.vector.memset(plane[:], 0)
         unit = tile("unit", [P, 1], F32)
         nc.vector.memset(unit[:], 1.0)
 
-        tab_first = tile("tab_first", [P, T], I32)
-        nc.sync.dma_start(tab_first[:], tab_words[0].rearrange("p t i -> p (t i)").bitcast(I32))
-        for q in range(4):
-            queue = nc.scalar if q else nc.sync
+        tab_win = [tile("tab%d" % a, [P, T], I32) for a in range(KP)]
+
+        def load_tab(a):
+            nc.sync.dma_start(tab_win[a][:], tab_words[a].rearrange("p t i -> p (t i)").bitcast(I32))
+
+        def load_tab_scales(queue, q):
             queue.dma_start(scale_win[32 * q : 32 * q + 4 * KP, :], tab_scales[:, 4 * q : 4 * q + 4, :].bitcast(I32))
 
         def load_w4_scales(queue, q):
             queue.dma_start(w4s_raw[32 * q : 32 * q + 4, :, :], w4_scales[:, 4 * q : 4 * q + 4, :].rearrange("a r c -> r a c").bitcast(I32))
 
+        load_tab(0)
         for q in range(4):
-            load_w4_scales(nc.scalar, q)
-        w4_raw = tile("w4_raw", [P, KP, H // 2], I32, 56 * KIB)
-        nc.sync.dma_start(w4_raw[:], w4_words.rearrange("a p c -> p a c").bitcast(I32))
-        tab_rest = tile("tab_rest", [P, KP - 1, T], I32)
-        nc.sync.dma_start(tab_rest[:], tab_words[1:].rearrange("a p t i -> p a (t i)").bitcast(I32))
-        tab_win = [tab_first[:], tab_rest[:, 0, :], tab_rest[:, 1, :]]
+            load_tab_scales(nc.scalar if q < 2 else nc.sync, q)
+        for q in range(4):
+            load_w4_scales(nc.scalar if q < 2 else nc.gpsimd, q)
+        w4_first = tile("w4_first", [P, H // 2], I32, W4_FIRST)
+        nc.sync.dma_start(w4_first[:], w4_words[0].bitcast(I32))
+        w4_rest = tile("w4_rest", [P, KP - 1, H // 2], I32)
+        nc.sync.dma_start(w4_rest[:], w4_words[1:].rearrange("a p c -> p a c").bitcast(I32))
+        load_tab(1)
+        load_tab(2)
 
         v_tiles = []
 
         def gather_tab(a, j0, j1, offset=None):
             picked = tile("v%d_%d" % (a, j0), [P, j1 - j0], U32, offset)
             v_tiles.append((a, j0, j1, picked))
-            nc.vector.tensor_copy(picked[:], tab_win[a].bitcast(U32).indirect(picks(j0, j1)))
+            nc.vector.tensor_copy(picked[:], tab_win[a][:].bitcast(U32).indirect(picks(j0, j1)))
 
         def v_cols(a, j0, j1):
             for pass_, lo, hi, picked in v_tiles:
@@ -85,50 +94,54 @@ def tile_list_pseudo_huber_reprojection_kernel(tc, tab_words, tab_scales, offs, 
                     return picked[:, j0 - lo : j1 - lo]
             raise ValueError("no tile")
 
-        v_scales = [tile("v_scales%d" % half, [P, HALF], U8, (None, 8 * KIB + 64)[half]) for half in range(2)]
+        v_scales = tile("v_scales", [P, S], U8)
 
         def gather_scales(half):
-            nc.vector.tensor_copy(v_scales[half][:], scale_win[:].bitcast(U8).indirect(picks(HALF * half, HALF * (half + 1))))
-            for a in range(1, KP):
-                nc.scalar.dma_start(moved[2 * half + a - 1][0:MOVE_ROWS, :], v_scales[half][4 * a : 4 * a + MOVE_ROWS, :].bitcast(I32))
+            nc.vector.tensor_copy(v_scales[:, HALF * half : HALF * (half + 1)], scale_win[:].bitcast(U8).indirect(picks(HALF * half, HALF * (half + 1))))
 
-        def v_plane(a, j0, j1):
-            half, lo = divmod(j0, HALF)
+        def move_scales(i):
+            a, j0, j1 = moves[i]
+            nc.sync.dma_start(moved[i][0:MOVE_ROWS, :], v_scales[4 * a : 4 * a + MOVE_ROWS, j0:j1].bitcast(I32))
+
+        def v_plane(a, j):
             if a == 0:
-                return v_scales[half][:, lo : lo + j1 - j0]
-            return moved[2 * half + a - 1][:, lo // 4 : (lo + j1 - j0) // 4].bitcast(U8)
+                return v_scales[:, j : j + P]
+            for plane, (pass_, j0, j1) in zip(moved, moves):
+                if pass_ == a and j0 <= j < j1:
+                    return plane[:, (j - j0) // 4 : (j - j0 + P) // 4].bitcast(U8)
+            raise ValueError("no plane")
 
+        one = tile("one", [P, 1], F32)
+        nc.scalar.activation(out=one[:], in_=unit[:], func=ACT.Sqrt)
         gather_tab(0, 0, HALF)
         gather_scales(0)
-        w4_codes = [tile("w4_codes%d" % a, [P, H // 2], I32, (None, 6 * KIB + 64, 11 * KIB - 64)[a]) for a in range(KP)]
-
-        def deal_w4(a):
-            nc.vector.tensor_copy(w4_codes[a][:].rearrange("p (b t q w) -> p b t q w", b=HP, t=4, q=16),
-                                  w4_raw[:, a, :].rearrange("p (b q t w) -> p b t q w", b=HP, t=4, q=16))
-
-        deal_w4(0)
-        w4_planes = tile("w4_planes", [P, KP, H // 4], I32)
-        nc.vector.tensor_copy(w4_planes[:].rearrange("p a (b t q w) -> p (a b) t q w", b=HP, t=4, q=16),
-                              w4s_raw[:].rearrange("p a (b q t w) -> p (a b) t q w", b=HP, t=4, q=16))
-        one = tile("one", [P, 1], F32, 8 * KIB + 2624)
-        nc.scalar.activation(out=one[:], in_=unit[:], func=ACT.Sqrt)
-        deal_w4(1)
-        deal_w4(2)
+        move_scales(0)
         gather_scales(1)
-        gather_tab(0, HALF, S, 8 * KIB + 576)
+        gather_tab(0, HALF, S, SCALE_WIN)
+        move_scales(1)
+        w4_codes = [tile("w4_codes%d" % a, [P, H // 2], I32, (None, W4_SCALES, W4_SCALES + 2 * KIB)[a]) for a in range(KP)]
+        w4_planes = [tile("w4_planes%d" % a, [P, H // 4], I32, (None, W4_FIRST, W4_FIRST + KIB)[a]) for a in range(KP)]
 
-        g_win = [tile("g_win%d" % m, [P, T], F32) for m in range(NT)]
+        def deal(dealt, raw):
+            nc.scalar.copy(dealt.bitcast(U32).rearrange("p (b t q w) -> p b t q w", b=HP, t=4, q=16),
+                           raw.bitcast(U32).rearrange("p (b q t w) -> p b t q w", b=HP, t=4, q=16))
 
-        def load_g(m):
-            nc.sync.dma_start(g_win[m][:], gT[P * m : P * (m + 1), :])
+        deal(w4_codes[0][:], w4_first[:])
+        for a in range(KP):
+            deal(w4_planes[a][:], w4s_raw[:, a, :])
+        for a in range(1, KP):
+            deal(w4_codes[a][:], w4_rest[:, a - 1, :])
 
-        w2_raw = [tile("w2_raw%d" % b, [P, 4, N], F32, (56 * KIB, None)[b]) for b in range(HP)]
+        w2_raw = [tile("w2_raw%d" % b, [P, 4, N], F32, (None, W2_RAW)[b]) for b in range(HP)]
         w2_rows = w2.rearrange("(b q t i) n -> b t q i n", b=HP, q=16, t=4)
         for b in range(HP):
             for t in range(4):
                 nc.sync.dma_start(w2_raw[b][:, t, :], w2_rows[b, t])
+                if (b, t) == (0, 1):
+                    move_scales(2)
+        g_win = [tile("g_win%d" % m, [P, T], F32) for m in range(NT)]
         for m in range(NT):
-            load_g(m)
+            nc.sync.dma_start(g_win[m][:], gT[P * m : P * (m + 1), :])
 
         def bank_tile(shape, bank):
             return psum.tile(shape, F32, name="bank", tag="bank%d" % bank)
@@ -139,150 +152,147 @@ def tile_list_pseudo_huber_reprojection_kernel(tc, tab_words, tab_scales, offs, 
                     nc.tensor.matmul_mx(
                         out=bank[:, t, :],
                         lhsT=w4_codes[a][:, 256 * b + 64 * t : 256 * b + 64 * (t + 1)].bitcast(U8).bitcast(FP4X4),
-                        lhsT_scale=w4_planes[:, a, 128 * b + 32 * t : 128 * b + 32 * (t + 1)].bitcast(U8),
+                        lhsT_scale=w4_planes[a][:, 128 * b + 32 * t : 128 * b + 32 * (t + 1)].bitcast(U8),
                         rhs=v_cols(a, j, j + P).bitcast(FP8X4),
-                        rhs_scale=v_plane(a, j, j + P),
+                        rhs_scale=v_plane(a, j),
                         start=(a == 0 and t == 0),
                         stop=(a == KP - 1 and t == 3),
                     )
 
         def relu(grouped, bank, j):
-            nc.scalar.activation(out=grouped[:, j % grouped.shape[1] : j % grouped.shape[1] + P, :], in_=bank[:].rearrange("p t j -> p j t"), func=ACT.Relu)
+            lo = j % grouped.shape[1]
+            nc.scalar.activation(out=grouped[:, lo : lo + P, :], in_=bank[:].rearrange("p t j -> p j t"), func=ACT.Relu)
 
         h_scales = tile("h_scales", [P, HP, S], U8)
 
-        def quantize_h(codes, grouped, b, j0):
-            nc.vector.quantize_mx(out=codes.bitcast(FP8X4), scales=h_scales[:, b, j0 : j0 + grouped.shape[1]],
+        def quantize_h(grouped, b, j0, offset=None):
+            width = grouped.shape[1]
+            codes = tile("h_codes%d_%d" % (b, j0), [P, width], U32, offset)
+            nc.vector.quantize_mx(out=codes[:].bitcast(FP8X4), scales=h_scales[:, b, j0 : j0 + width],
                                   in_=grouped[:].rearrange("p j t -> p (j t)"))
+            return codes
 
         early = [(b, j0 + j) for j0 in (0, QUARTER) for b in range(HP) for j in (0, P)]
-        early_banks = [bank_tile([P, 4, P], i) for i in range(BANKS)]
+        early_banks = [bank_tile([P, 4, P], i) for i in range(8)]
         for bank, (b, j) in zip(early_banks, early):
             decode_passes(bank, b, j, [0])
-        for j0, j1 in ((0, QUARTER), (QUARTER, HALF), (HALF, S)):
-            for a in range(1, KP):
-                gather_tab(a, j0, j1)
-        w2_codes = tile("w2_codes", [P, HP, N], U32)
+        gather_tab(1, 0, HALF)
+        gather_tab(1, HALF, S)
+        for j0 in (0, QUARTER, THIRD, FOURTH):
+            gather_tab(2, j0, j0 + QUARTER)
+        first_h = [tile("first_h%d" % b, [P, HALF, 4], BF16) for b in range(HP)]
+        for bank, (b, j) in zip(early_banks, early):
+            decode_passes(bank, b, j, [1, 2])
+            relu(first_h[b], bank, j)
+
+        w2_codes = [tile("w2_codes%d" % b, [P, N], U32) for b in range(HP)]
         w2_scales = tile("w2_scales", [P, HP, N], U8)
 
-        def quantize_w2(b, copy):
-            grouped = tile("w2_grouped%d" % b, [P, N, 4], BF16)
-            copy(grouped[:].rearrange("p (c i) t -> p c t i", i=4), w2_raw[b][:].rearrange("p t (c i) -> p c t i", i=4))
-            nc.vector.quantize_mx(out=w2_codes[:, b, :].bitcast(FP8X4), scales=w2_scales[:, b, :],
-                                  in_=grouped[:].rearrange("p n t -> p (n t)"))
+        w2_rounded = [tile("w2_rounded%d" % b, [P, N, 4], BF16) for b in range(HP)]
 
-        first_codes = [tile("first_codes%d" % b, [P, HALF], U32) for b in range(HP)]
-        first_h = [tile("first_h%d" % b, [P, HALF, 4], BF16) for b in range(HP)]
-        for i, (bank, (b, j)) in enumerate(zip(early_banks, early)):
-            if i == 0:
-                decode_passes(bank, b, j, [1])
-                decode_passes(early_banks[1], early[1][0], early[1][1], [1])
-            decode_passes(bank, b, j, [2] if i < 2 else [1, 2])
-            relu(first_h[b], bank, j)
-        for b in range(HP):
-            quantize_h(first_codes[b][:], first_h[b], b, 0)
-        quantize_w2(0, nc.vector.tensor_copy)
-        quantize_w2(1, nc.scalar.copy)
+        def round_w2(copy, b, n0, n1):
+            copy(w2_rounded[b][:, n0:n1, :].rearrange("p (c i) t -> p c t i", i=4), w2_raw[b][:, :, n0:n1].rearrange("p t (c i) -> p c t i", i=4))
 
-        def project(bank_number, rows, j0, codes):
-            width = codes[0].shape[1]
-            bank = bank_tile([P, len(rows), width], bank_number)
-            for i, m in enumerate(rows):
-                for b in range(HP):
+        def quantize_w2(b):
+            nc.vector.quantize_mx(out=w2_codes[b][:].bitcast(FP8X4), scales=w2_scales[:, b, :],
+                                  in_=w2_rounded[b][:].rearrange("p n t -> p (n t)"))
+
+        round_w2(nc.vector.tensor_copy, 0, 0, N)
+        quantize_w2(0)
+        round_w2(nc.vector.tensor_copy, 1, 0, N // 2)
+        round_w2(nc.scalar.copy, 1, N // 2, N)
+        first_codes = [quantize_h(first_h[b], b, 0) for b in range(HP)]
+        quantize_w2(1)
+
+        def project(bank, rows, j0, codes, passes):
+            width = bank.shape[2]
+            for b in passes:
+                for i, m in enumerate(rows):
                     nc.tensor.matmul_mx(
                         out=bank[:, i, :],
-                        lhsT=w2_codes[:, b, P * m : P * (m + 1)].bitcast(FP8X4),
+                        lhsT=w2_codes[b][:, P * m : P * (m + 1)].bitcast(FP8X4),
                         lhsT_scale=w2_scales[:, b, P * m : P * (m + 1)],
                         rhs=codes[b][:].bitcast(FP8X4),
                         rhs_scale=h_scales[:, b, j0 : j0 + width],
-                        start=(b == 0),
-                        stop=(b == HP - 1),
+                        start=(b == 0 and i == 0),
+                        stop=(b == HP - 1 and i == len(rows) - 1),
                     )
-            return bank
 
-        def project_half(bank, rows, j0, codes, b):
-            for i, m in enumerate(rows):
-                nc.tensor.matmul_mx(
-                    out=bank[:, i, :],
-                    lhsT=w2_codes[:, b, P * m : P * (m + 1)].bitcast(FP8X4),
-                    lhsT_scale=w2_scales[:, b, P * m : P * (m + 1)],
-                    rhs=codes[b][:].bitcast(FP8X4),
-                    rhs_scale=h_scales[:, b, j0 : j0 + QUARTER],
-                    start=(b == 0 and i == 0),
-                    stop=(b == HP - 1 and i == len(rows) - 1),
-                )
-
-        def decode_late(b, j0, banks, offset=None):
-            grouped = tile("h%d_%d" % (b, j0), [P, QUARTER, 4], BF16, offset)
-            for i, j in enumerate((j0, j0 + P)):
-                bank = bank_tile([P, 4, P], banks[i])
-                decode_passes(bank, b, j, range(KP))
-                relu(grouped, bank, j)
-            return grouped
+        def decode(grouped, b, j, number):
+            bank = bank_tile([P, 4, P], number)
+            decode_passes(bank, b, j, range(KP))
+            relu(grouped, bank, j)
 
         out_rows = out.rearrange("(m p) j -> p m j", p=P)
 
-        def finish(res, m0, j0, last):
+        def finish(res, m0, j0, square, minus_one):
             rows, width = res.shape[1], res.shape[2]
-            if last and m0:
-                nc.vector.tensor_tensor(res[:], res[:], res[:], ALU.mult)
-            else:
+            if square is nc.scalar:
                 nc.scalar.activation(out=res[:], in_=res[:], func=ACT.Square)
+            else:
+                square.tensor_tensor(res[:], res[:], res[:], ALU.mult)
             nc.scalar.activation(out=res[:], in_=res[:], func=ACT.Sqrt, bias=one[:])
-            (nc.vector if last else nc.gpsimd).tensor_scalar(res[:], res[:], 1.0, -1.0, ALU.mult, ALU.add)
+            minus_one.tensor_scalar(res[:], res[:], 1.0, -1.0, ALU.mult, ALU.add)
             nc.sync.dma_start(out_rows[:, m0 : m0 + rows, j0 : j0 + width], res[:])
-
-        def evacuate(bank, m, offset=None):
-            predicted = tile("p%d" % m, [P, HALF], F32, offset)
-            nc.scalar.copy(predicted[:], bank[:, 0, :])
-            return predicted
 
         def finish_fused(m):
             res = tile("res%d" % m, [P, 1, HALF], F32)
             nc.vector.tensor_tensor(res[:, 0, :], g_win[m][:].indirect(picks(0, HALF)), first[m][:], ALU.subtract)
-            finish(res, m, 0, False)
+            finish(res, m, 0, nc.scalar, nc.gpsimd)
 
-        def finish_gathered(bank, observed, m0, j0, last, offset=None):
-            res = tile("res%d_%d" % (m0, j0), list(bank.shape), F32, offset)
-            nc.vector.tensor_tensor(res[:], bank[:], observed, ALU.subtract)
-            finish(res, m0, j0, last)
-
-        THIRD, FOURTH = HALF, HALF + QUARTER
-        g_low = tile("g_low", [P, 2, HALF], F32)
-        g_third = tile("g_third", [P, 2, QUARTER], F32)
-        g_fourth = tile("g_fourth", [P, 2, QUARTER], F32, 42 * KIB)
+        def finish_gathered(predicted, observed, m0, j0, square, minus_one, offset=None):
+            res = tile("res%d_%d" % (m0, j0), list(predicted.shape), F32, offset)
+            nc.vector.tensor_tensor(res[:], predicted, observed, ALU.subtract)
+            finish(res, m0, j0, square, minus_one)
 
         def gather_g(picked, m, j0):
             nc.vector.tensor_copy(picked, g_win[m][:].indirect(picks(j0, j0 + picked.shape[1])))
 
-        third_codes = [tile("third_codes%d" % b, [P, QUARTER], U32) for b in range(HP)]
-        fourth_codes = [tile("fourth_codes%d" % b, [P, QUARTER], U32) for b in range(HP)]
-        gather_g(g_low[:, 0, :], 0, HALF)
-        third_h = [decode_late(b, THIRD, (2 * b, 2 * b + 1)) for b in range(HP)]
-        first_banks = [project(4 + m, [m], 0, first_codes) for m in range(NT)]
-        first = {m: evacuate(first_banks[m], m) for m in range(NT)}
+        third_h = [tile("h%d_%d" % (b, THIRD), [P, QUARTER, 4], BF16, (W2_RAW, None)[b]) for b in range(HP)]
+        decode(third_h[0], 0, THIRD, 0)
+        first_banks = [bank_tile([P, 1, HALF], 2 + m) for m in range(NT)]
         for b in range(HP):
-            quantize_h(third_codes[b][:], third_h[b], b, THIRD)
-        third_low = project(0, [0, 1], THIRD, third_codes)
-        gather_g(g_low[:, 1, :], 1, HALF)
+            for m in range(NT):
+                project(first_banks[m], [m], 0, first_codes, [b])
+        first = []
+        for m in range(NT):
+            predicted = tile("p%d" % m, [P, HALF], F32, (None, COPY_OF_P, None, COPY_OF_LAST_P)[m])
+            nc.scalar.copy(predicted[:], first_banks[m][:, 0, :])
+            first.append(predicted)
+        decode(third_h[0], 0, THIRD + P, 2)
+        decode(third_h[1], 1, THIRD, 3)
+        decode(third_h[1], 1, THIRD + P, 4)
+
+        g_low = tile("g_low", [P, 2, HALF], F32)
+        gather_g(g_low[:, 0, :], 0, HALF)
         finish_fused(0)
-        fourth_h = [decode_late(0, FOURTH, (4, 5)), decode_late(1, FOURTH, (6, 7), 41 * KIB)]
         finish_fused(1)
-        finish_gathered(third_low, g_low[:, :, :QUARTER], 0, THIRD, False)
-        gather_g(g_third[:, 0, :], 2, THIRD)
+        gather_g(g_low[:, 1, :], 1, HALF)
+        third_codes = [quantize_h(third_h[b], b, THIRD, COPY_OF_P + KIB * b) for b in range(HP)]
+        fourth_h = [tile("h%d_%d" % (b, FOURTH), [P, QUARTER, 4], BF16, (None, LAST_H)[b]) for b in range(HP)]
+        decode(fourth_h[0], 0, FOURTH, 5)
+        decode(fourth_h[0], 0, FOURTH + P, 2)
+        third = [bank_tile([P, 2, QUARTER], i) for i in range(2)]
+        for i in range(2):
+            project(third[i], [2 * i, 2 * i + 1], THIRD, third_codes, range(HP))
+        decode(fourth_h[1], 1, FOURTH, 3)
+        decode(fourth_h[1], 1, FOURTH + P, 4)
         finish_fused(2)
-        quantize_h(fourth_codes[0][:], fourth_h[0], 0, FOURTH)
-        third_high = project(6, [2, 3], THIRD, third_codes)
-        fourth = [bank_tile([P, 2, QUARTER], 2 + i) for i in range(2)]
-        for i in range(2):
-            project_half(fourth[i], [2 * i, 2 * i + 1], FOURTH, fourth_codes, 0)
-        gather_g(g_third[:, 1, :], 3, THIRD)
+        g_third = tile("g_third", [P, 2, QUARTER], F32)
+        gather_g(g_third[:, 0, :], 2, THIRD)
+        fourth_codes = [quantize_h(fourth_h[0], 0, FOURTH)]
         finish_fused(3)
-        quantize_h(fourth_codes[1][:], fourth_h[1], 1, FOURTH)
-        for i in range(2):
-            project_half(fourth[i], [2 * i, 2 * i + 1], FOURTH, fourth_codes, 1)
-        finish_gathered(third_high, g_third[:], 2, THIRD, False, 44 * KIB)
+        gather_g(g_third[:, 1, :], 3, THIRD)
+        fourth_codes.append(quantize_h(fourth_h[1], 1, FOURTH))
+        fourth = [bank_tile([P, 2, QUARTER], 6 + i) for i in range(2)]
+        for b in range(HP):
+            for i in range(2):
+                project(fourth[i], [2 * i, 2 * i + 1], FOURTH, fourth_codes, [b])
+        finish_gathered(third[0][:], g_low[:, :, :QUARTER], 0, THIRD, nc.scalar, nc.gpsimd, COPY_OF_LAST_P)
+        finish_gathered(third[1][:], g_third[:], 2, THIRD, nc.scalar, nc.gpsimd)
+        g_fourth = tile("g_fourth", [P, 2, QUARTER], F32, LAST_H)
         gather_g(g_fourth[:, 0, :], 2, FOURTH)
-        finish_gathered(fourth[0], g_low[:, :, QUARTER:], 0, FOURTH, True)
+        finish_gathered(fourth[0][:], g_low[:, :, QUARTER:], 0, FOURTH, nc.scalar, nc.vector)
+        finish_gathered(fourth[1][:, 0:1, :], g_fourth[:, 0:1, :], 2, FOURTH, nc.vector, nc.vector)
         gather_g(g_fourth[:, 1, :], 3, FOURTH)
-        finish_gathered(fourth[1], g_fourth[:], 2, FOURTH, True)
+        finish_gathered(fourth[1][:, 1:2, :], g_fourth[:, 1:2, :], 3, FOURTH, nc.vector, nc.vector)

@@ -39,7 +39,7 @@ def tile_list_pseudo_huber_reprojection_kernel(tc, tab_words, tab_scales, offs, 
                 return held.tile(shape, dtype, name=name, align_bytes=64)
             return shared.tile(shape, dtype, name=name, offset=offset, align_bytes=64)
 
-        SCALE_WIN, COPY_OF_P, LAST_H, W4_SCALES, COPY_OF_LAST_P, W4_FIRST, W2_RAW = 0, 2 * KIB, 4 * KIB, 6 * KIB, 10 * KIB, 12 * KIB, 14 * KIB
+        COPY_OF_P, LAST_H, W4_SCALES, W4_FIRST, W2_RAW = 0, 2 * KIB, 4 * KIB, 9 * KIB, 13 * KIB
 
         offsets = held.tile([P, S // 16], U16, name="offsets")
         nc.sync.dma_start(offsets[:], offs)
@@ -47,7 +47,7 @@ def tile_list_pseudo_huber_reprojection_kernel(tc, tab_words, tab_scales, offs, 
         def picks(j0, j1):
             return offsets[:, j0 // 16 : j1 // 16]
 
-        scale_win = tile("scale_win", [P, T // 4], I32, SCALE_WIN)
+        scale_win = tile("scale_win", [P, T // 4], I32)
         nc.gpsimd.memset(scale_win[:], 0)
         w4s_raw = tile("w4s_raw", [P, KP, H // 4], I32, W4_SCALES)
         nc.vector.memset(w4s_raw[:], 0)
@@ -117,10 +117,10 @@ def tile_list_pseudo_huber_reprojection_kernel(tc, tab_words, tab_scales, offs, 
         gather_scales(0)
         move_scales(0)
         gather_scales(1)
-        gather_tab(0, HALF, S, SCALE_WIN)
+        gather_tab(0, HALF, S, W4_FIRST + KIB + 64)
         move_scales(1)
         w4_codes = [tile("w4_codes%d" % a, [P, H // 2], I32, (None, W4_SCALES, W4_SCALES + 2 * KIB)[a]) for a in range(KP)]
-        w4_planes = [tile("w4_planes%d" % a, [P, H // 4], I32, (None, W4_FIRST, W4_FIRST + KIB)[a]) for a in range(KP)]
+        w4_planes = [tile("w4_planes%d" % a, [P, H // 4], I32, (None, W4_FIRST - KIB + 64, W4_FIRST + 64)[a]) for a in range(KP)]
 
         def deal(dealt, raw):
             nc.scalar.copy(dealt.bitcast(U32).rearrange("p (b t q w) -> p b t q w", b=HP, t=4, q=16),
@@ -178,8 +178,8 @@ def tile_list_pseudo_huber_reprojection_kernel(tc, tab_words, tab_scales, offs, 
             decode_passes(bank, b, j, [0])
         gather_tab(1, 0, HALF)
         gather_tab(1, HALF, S)
-        for j0 in (0, QUARTER, THIRD, FOURTH):
-            gather_tab(2, j0, j0 + QUARTER)
+        for j0, j1 in ((0, QUARTER), (QUARTER, HALF), (HALF, S)):
+            gather_tab(2, j0, j1)
         first_h = [tile("first_h%d" % b, [P, HALF, 4], BF16) for b in range(HP)]
         for bank, (b, j) in zip(early_banks, early):
             decode_passes(bank, b, j, [1, 2])
@@ -190,19 +190,15 @@ def tile_list_pseudo_huber_reprojection_kernel(tc, tab_words, tab_scales, offs, 
 
         w2_rounded = [tile("w2_rounded%d" % b, [P, N, 4], BF16) for b in range(HP)]
 
-        def round_w2(copy, b, n0, n1):
-            copy(w2_rounded[b][:, n0:n1, :].rearrange("p (c i) t -> p c t i", i=4), w2_raw[b][:, :, n0:n1].rearrange("p t (c i) -> p c t i", i=4))
-
-        def quantize_w2(b):
-            nc.vector.quantize_mx(out=w2_codes[b][:].bitcast(FP8X4), scales=w2_scales[:, b, :],
-                                  in_=w2_rounded[b][:].rearrange("p n t -> p (n t)"))
-
-        round_w2(nc.vector.tensor_copy, 0, 0, N)
-        quantize_w2(0)
-        round_w2(nc.vector.tensor_copy, 1, 0, N // 2)
-        round_w2(nc.scalar.copy, 1, N // 2, N)
-        first_codes = [quantize_h(first_h[b], b, 0) for b in range(HP)]
-        quantize_w2(1)
+        halves = (slice(0, N // 2), slice(N // 2, N))
+        for b in range(HP):
+            for cols in halves:
+                nc.vector.tensor_copy(w2_rounded[b][:, cols, :].rearrange("p (c i) t -> p c t i", i=4),
+                                      w2_raw[b][:, :, cols].rearrange("p t (c i) -> p c t i", i=4))
+            for cols in halves:
+                nc.vector.quantize_mx(out=w2_codes[b][:, cols].bitcast(FP8X4), scales=w2_scales[:, b, cols],
+                                      in_=w2_rounded[b][:, cols, :].rearrange("p n t -> p (n t)"))
+        first_codes = [quantize_h(first_h[b], b, 0, W2_RAW + 2 * KIB * b) for b in range(HP)]
 
         def project(bank, rows, j0, codes, passes):
             width = bank.shape[2]
@@ -248,47 +244,45 @@ def tile_list_pseudo_huber_reprojection_kernel(tc, tab_words, tab_scales, offs, 
         def gather_g(picked, m, j0):
             nc.vector.tensor_copy(picked, g_win[m][:].indirect(picks(j0, j0 + picked.shape[1])))
 
-        third_h = [tile("h%d_%d" % (b, THIRD), [P, QUARTER, 4], BF16, (W2_RAW, None)[b]) for b in range(HP)]
+        third_h = [tile("h%d_%d" % (b, THIRD), [P, QUARTER, 4], BF16) for b in range(HP)]
         decode(third_h[0], 0, THIRD, 0)
+        decode(third_h[0], 0, THIRD + P, 1)
+        decode(third_h[1], 1, THIRD, 6)
         first_banks = [bank_tile([P, 1, HALF], 2 + m) for m in range(NT)]
-        for b in range(HP):
-            for m in range(NT):
-                project(first_banks[m], [m], 0, first_codes, [b])
         first = []
         for m in range(NT):
-            predicted = tile("p%d" % m, [P, HALF], F32, (None, COPY_OF_P, None, COPY_OF_LAST_P)[m])
+            project(first_banks[m], [m], 0, first_codes, range(HP))
+            predicted = tile("p%d" % m, [P, HALF], F32, COPY_OF_P if m == 1 else None)
             nc.scalar.copy(predicted[:], first_banks[m][:, 0, :])
             first.append(predicted)
-        decode(third_h[0], 0, THIRD + P, 2)
-        decode(third_h[1], 1, THIRD, 3)
-        decode(third_h[1], 1, THIRD + P, 4)
 
         g_low = tile("g_low", [P, 2, HALF], F32)
         gather_g(g_low[:, 0, :], 0, HALF)
         finish_fused(0)
+        decode(third_h[1], 1, THIRD + P, 2)
         finish_fused(1)
         gather_g(g_low[:, 1, :], 1, HALF)
         third_codes = [quantize_h(third_h[b], b, THIRD, COPY_OF_P + KIB * b) for b in range(HP)]
         fourth_h = [tile("h%d_%d" % (b, FOURTH), [P, QUARTER, 4], BF16, (None, LAST_H)[b]) for b in range(HP)]
-        decode(fourth_h[0], 0, FOURTH, 5)
-        decode(fourth_h[0], 0, FOURTH + P, 2)
+        decode(fourth_h[0], 0, FOURTH, 3)
+        decode(fourth_h[0], 0, FOURTH + P, 4)
+        decode(fourth_h[1], 1, FOURTH, 5)
+        decode(fourth_h[1], 1, FOURTH + P, 2)
         third = [bank_tile([P, 2, QUARTER], i) for i in range(2)]
         for i in range(2):
             project(third[i], [2 * i, 2 * i + 1], THIRD, third_codes, range(HP))
-        decode(fourth_h[1], 1, FOURTH, 3)
-        decode(fourth_h[1], 1, FOURTH + P, 4)
         finish_fused(2)
         g_third = tile("g_third", [P, 2, QUARTER], F32)
         gather_g(g_third[:, 0, :], 2, THIRD)
         fourth_codes = [quantize_h(fourth_h[0], 0, FOURTH)]
         finish_fused(3)
-        gather_g(g_third[:, 1, :], 3, THIRD)
         fourth_codes.append(quantize_h(fourth_h[1], 1, FOURTH))
+        gather_g(g_third[:, 1, :], 3, THIRD)
         fourth = [bank_tile([P, 2, QUARTER], 6 + i) for i in range(2)]
         for b in range(HP):
             for i in range(2):
                 project(fourth[i], [2 * i, 2 * i + 1], FOURTH, fourth_codes, [b])
-        finish_gathered(third[0][:], g_low[:, :, :QUARTER], 0, THIRD, nc.scalar, nc.gpsimd, COPY_OF_LAST_P)
+        finish_gathered(third[0][:], g_low[:, :, :QUARTER], 0, THIRD, nc.scalar, nc.gpsimd)
         finish_gathered(third[1][:], g_third[:], 2, THIRD, nc.scalar, nc.gpsimd)
         g_fourth = tile("g_fourth", [P, 2, QUARTER], F32, LAST_H)
         gather_g(g_fourth[:, 0, :], 2, FOURTH)

@@ -57,6 +57,7 @@ def tile_list_pseudo_huber_reprojection_kernel(tc, tab_words, tab_scales, offs, 
             nc.vector.memset(plane[:], 0)
         unit = tile("unit", [P, 1], F32)
         nc.vector.memset(unit[:], 1.0)
+        one = tile("one", [P, 1], F32)
 
         tab_win = [tile("tab%d" % a, [P, T], I32) for a in range(KP)]
 
@@ -73,7 +74,9 @@ def tile_list_pseudo_huber_reprojection_kernel(tc, tab_words, tab_scales, offs, 
         for q in range(4):
             load_tab_scales(nc.scalar if q < 2 else nc.sync, q)
         for q in range(4):
-            load_w4_scales(nc.scalar if q < 2 else nc.gpsimd, q)
+            load_w4_scales(nc.scalar, q)
+            if q == 1:
+                nc.scalar.activation(out=one[:], in_=unit[:], func=ACT.Sqrt)
         w4_first = tile("w4_first", [P, H // 2], I32, W4_FIRST)
         nc.sync.dma_start(w4_first[:], w4_words[0].bitcast(I32))
         w4_rest = tile("w4_rest", [P, KP - 1, H // 2], I32)
@@ -111,8 +114,6 @@ def tile_list_pseudo_huber_reprojection_kernel(tc, tab_words, tab_scales, offs, 
                     return plane[:, (j - j0) // 4 : (j - j0 + P) // 4].bitcast(U8)
             raise ValueError("no plane")
 
-        one = tile("one", [P, 1], F32)
-        nc.scalar.activation(out=one[:], in_=unit[:], func=ACT.Sqrt)
         gather_tab(0, 0, HALF)
         gather_scales(0)
         move_scales(0)

@@ -39,7 +39,7 @@ def tile_list_pseudo_huber_reprojection_kernel(tc, tab_words, tab_scales, offs, 
                 return held.tile(shape, dtype, name=name, align_bytes=64)
             return shared.tile(shape, dtype, name=name, offset=offset, align_bytes=64)
 
-        COPY_OF_P, LAST_H, W4_SCALES, W4_FIRST, W2_RAW = 0, 2 * KIB, 4 * KIB, 9 * KIB, 13 * KIB
+        COPY_OF_P, LAST_H, W4_SCALES, W4_FIRST, W2_RAW, G_HIGH = 0, 2 * KIB, 4 * KIB, 10 * KIB, 14 * KIB, 22 * KIB
 
         offsets = held.tile([P, S // 16], U16, name="offsets")
         nc.sync.dma_start(offsets[:], offs)
@@ -51,7 +51,7 @@ def tile_list_pseudo_huber_reprojection_kernel(tc, tab_words, tab_scales, offs, 
         nc.gpsimd.memset(scale_win[:], 0)
         w4s_raw = tile("w4s_raw", [P, KP, H // 4], I32, W4_SCALES)
         nc.vector.memset(w4s_raw[:], 0)
-        moves = [(1, 0, HALF), (2, 0, S), (1, HALF, S)]
+        moves = [(1, 0, QUARTER), (2, 0, S), (1, QUARTER, S)]
         moved = [tile("moved%d" % i, [P, (j1 - j0) // 4], I32) for i, (a, j0, j1) in enumerate(moves)]
         for plane in moved:
             nc.vector.memset(plane[:], 0)
@@ -79,10 +79,9 @@ def tile_list_pseudo_huber_reprojection_kernel(tc, tab_words, tab_scales, offs, 
                 nc.scalar.activation(out=one[:], in_=unit[:], func=ACT.Sqrt)
         w4_first = tile("w4_first", [P, H // 2], I32, W4_FIRST)
         nc.sync.dma_start(w4_first[:], w4_words[0].bitcast(I32))
-        w4_rest = tile("w4_rest", [P, KP - 1, H // 2], I32)
-        nc.sync.dma_start(w4_rest[:], w4_words[1:].rearrange("a p c -> p a c").bitcast(I32))
+        w4_rest = [tile("w4_rest%d" % a, [P, H // 2], I32) for a in range(1, KP)]
+        nc.sync.dma_start(w4_rest[0][:], w4_words[1].bitcast(I32))
         load_tab(1)
-        load_tab(2)
 
         v_tiles = []
 
@@ -99,8 +98,8 @@ def tile_list_pseudo_huber_reprojection_kernel(tc, tab_words, tab_scales, offs, 
 
         v_scales = tile("v_scales", [P, S], U8)
 
-        def gather_scales(half):
-            nc.vector.tensor_copy(v_scales[:, HALF * half : HALF * (half + 1)], scale_win[:].bitcast(U8).indirect(picks(HALF * half, HALF * (half + 1))))
+        def gather_scales(j0, j1):
+            nc.vector.tensor_copy(v_scales[:, j0:j1], scale_win[:].bitcast(U8).indirect(picks(j0, j1)))
 
         def move_scales(i):
             a, j0, j1 = moves[i]
@@ -114,32 +113,38 @@ def tile_list_pseudo_huber_reprojection_kernel(tc, tab_words, tab_scales, offs, 
                     return plane[:, (j - j0) // 4 : (j - j0 + P) // 4].bitcast(U8)
             raise ValueError("no plane")
 
-        gather_tab(0, 0, HALF)
-        gather_scales(0)
+        gather_tab(0, 0, QUARTER)
+        gather_scales(0, QUARTER)
         move_scales(0)
-        gather_scales(1)
+        load_tab(2)
+        gather_scales(QUARTER, S)
+        gather_tab(0, QUARTER, HALF, W4_FIRST + 64)
         gather_tab(0, HALF, S, W4_FIRST + KIB + 64)
         move_scales(1)
+        nc.sync.dma_start(w4_rest[1][:], w4_words[2].bitcast(I32))
+        move_scales(2)
         w4_codes = [tile("w4_codes%d" % a, [P, H // 2], I32, (None, W4_SCALES, W4_SCALES + 2 * KIB)[a]) for a in range(KP)]
-        w4_planes = [tile("w4_planes%d" % a, [P, H // 4], I32, (None, W4_FIRST - KIB + 64, W4_FIRST + 64)[a]) for a in range(KP)]
+        plane_first = tile("plane_first", [P, H // 4], I32)
+        planes_rest = tile("planes_rest", [P, KP - 1, H // 4], I32, W4_FIRST - 2 * KIB + 64)
+        w4_planes = [plane_first[:], planes_rest[:, 0, :], planes_rest[:, 1, :]]
 
-        def deal(dealt, raw):
-            nc.scalar.copy(dealt.bitcast(U32).rearrange("p (b t q w) -> p b t q w", b=HP, t=4, q=16),
-                           raw.bitcast(U32).rearrange("p (b q t w) -> p b t q w", b=HP, t=4, q=16))
+        def deal(dealt, raw, words):
+            nc.scalar.copy(dealt.bitcast(U32).rearrange("p (b t q w) -> p b t q w", t=4, q=16, w=words),
+                           raw.bitcast(U32).rearrange("p (b q t w) -> p b t q w", t=4, q=16, w=words))
 
-        deal(w4_codes[0][:], w4_first[:])
-        for a in range(KP):
-            deal(w4_planes[a][:], w4s_raw[:, a, :])
-        for a in range(1, KP):
-            deal(w4_codes[a][:], w4_rest[:, a - 1, :])
+        for b in range(HP):
+            deal(w4_codes[0][:, 256 * b : 256 * (b + 1)], w4_first[:, 256 * b : 256 * (b + 1)], 4)
+            deal(plane_first[:, 128 * b : 128 * (b + 1)], w4s_raw[:, 0, 128 * b : 128 * (b + 1)], 2)
+        deal(planes_rest[:].rearrange("p a c -> p (a c)"), w4s_raw[:, 1:, :].rearrange("p a c -> p (a c)"), 2)
+        deal(w4_codes[1][:], w4_rest[0][:], 4)
+        for b in range(HP):
+            deal(w4_codes[2][:, 256 * b : 256 * (b + 1)], w4_rest[1][:, 256 * b : 256 * (b + 1)], 4)
 
         w2_raw = [tile("w2_raw%d" % b, [P, 4, N], F32, (None, W2_RAW)[b]) for b in range(HP)]
         w2_rows = w2.rearrange("(b q t i) n -> b t q i n", b=HP, q=16, t=4)
         for b in range(HP):
             for t in range(4):
                 nc.sync.dma_start(w2_raw[b][:, t, :], w2_rows[b, t])
-                if (b, t) == (0, 1):
-                    move_scales(2)
         g_win = [tile("g_win%d" % m, [P, T], F32) for m in range(NT)]
         for m in range(NT):
             nc.sync.dma_start(g_win[m][:], gT[P * m : P * (m + 1), :])
@@ -177,8 +182,8 @@ def tile_list_pseudo_huber_reprojection_kernel(tc, tab_words, tab_scales, offs, 
         early_banks = [bank_tile([P, 4, P], i) for i in range(8)]
         for bank, (b, j) in zip(early_banks, early):
             decode_passes(bank, b, j, [0])
-        gather_tab(1, 0, HALF)
-        gather_tab(1, HALF, S)
+        gather_tab(1, 0, QUARTER)
+        gather_tab(1, QUARTER, S)
         for j0, j1 in ((0, QUARTER), (QUARTER, HALF), (HALF, S)):
             gather_tab(2, j0, j1)
         first_h = [tile("first_h%d" % b, [P, HALF, 4], BF16) for b in range(HP)]
@@ -192,14 +197,24 @@ def tile_list_pseudo_huber_reprojection_kernel(tc, tab_words, tab_scales, offs, 
         w2_rounded = [tile("w2_rounded%d" % b, [P, N, 4], BF16) for b in range(HP)]
 
         halves = (slice(0, N // 2), slice(N // 2, N))
-        for b in range(HP):
+
+        def round_w2(b):
             for cols in halves:
                 nc.vector.tensor_copy(w2_rounded[b][:, cols, :].rearrange("p (c i) t -> p c t i", i=4),
                                       w2_raw[b][:, :, cols].rearrange("p t (c i) -> p c t i", i=4))
-            for cols in halves:
-                nc.vector.quantize_mx(out=w2_codes[b][:, cols].bitcast(FP8X4), scales=w2_scales[:, b, cols],
-                                      in_=w2_rounded[b][:, cols, :].rearrange("p n t -> p (n t)"))
-        first_codes = [quantize_h(first_h[b], b, 0, W2_RAW + 2 * KIB * b) for b in range(HP)]
+
+        def quantize_w2(b, cols):
+            nc.vector.quantize_mx(out=w2_codes[b][:, cols].bitcast(FP8X4), scales=w2_scales[:, b, cols],
+                                  in_=w2_rounded[b][:, cols, :].rearrange("p n t -> p (n t)"))
+
+        round_w2(0)
+        for cols in halves:
+            quantize_w2(0, cols)
+        first_codes = [quantize_h(first_h[0], 0, 0)]
+        round_w2(1)
+        quantize_w2(1, halves[0])
+        first_codes.append(quantize_h(first_h[1], 1, 0, W2_RAW))
+        quantize_w2(1, halves[1])
 
         def project(bank, rows, j0, codes, passes):
             width = bank.shape[2]
@@ -273,21 +288,22 @@ def tile_list_pseudo_huber_reprojection_kernel(tc, tab_words, tab_scales, offs, 
         for i in range(2):
             project(third[i], [2 * i, 2 * i + 1], THIRD, third_codes, range(HP))
         finish_fused(2)
-        g_third = tile("g_third", [P, 2, QUARTER], F32)
-        gather_g(g_third[:, 0, :], 2, THIRD)
-        fourth_codes = [quantize_h(fourth_h[0], 0, FOURTH)]
-        finish_fused(3)
-        fourth_codes.append(quantize_h(fourth_h[1], 1, FOURTH))
-        gather_g(g_third[:, 1, :], 3, THIRD)
+        g_high = [tile("g_high%d" % i, [P, 1, HALF], F32, (G_HIGH, LAST_H)[i]) for i in range(2)]
+        gather_g(g_high[0][:, 0, :], 2, HALF)
+        fourth_codes = [quantize_h(fourth_h[b], b, FOURTH) for b in range(HP)]
         fourth = [bank_tile([P, 2, QUARTER], 6 + i) for i in range(2)]
         for b in range(HP):
             for i in range(2):
                 project(fourth[i], [2 * i, 2 * i + 1], FOURTH, fourth_codes, [b])
         finish_gathered(third[0][:], g_low[:, :, :QUARTER], 0, THIRD, nc.scalar, nc.gpsimd)
-        finish_gathered(third[1][:], g_third[:], 2, THIRD, nc.scalar, nc.gpsimd)
-        g_fourth = tile("g_fourth", [P, 2, QUARTER], F32, LAST_H)
-        gather_g(g_fourth[:, 0, :], 2, FOURTH)
-        finish_gathered(fourth[0][:], g_low[:, :, QUARTER:], 0, FOURTH, nc.scalar, nc.vector)
-        finish_gathered(fourth[1][:, 0:1, :], g_fourth[:, 0:1, :], 2, FOURTH, nc.vector, nc.vector)
-        gather_g(g_fourth[:, 1, :], 3, FOURTH)
-        finish_gathered(fourth[1][:, 1:2, :], g_fourth[:, 1:2, :], 3, FOURTH, nc.vector, nc.vector)
+        finish_fused(3)
+        finish_gathered(fourth[0][:], g_low[:, :, QUARTER:], 0, FOURTH, nc.scalar, nc.gpsimd)
+        res = tile("res_high", [P, 1, HALF], F32)
+        nc.vector.tensor_tensor(res[:, :, :QUARTER], third[1][:, 0:1, :], g_high[0][:, :, :QUARTER], ALU.subtract)
+        nc.vector.tensor_tensor(res[:, :, QUARTER:], fourth[1][:, 0:1, :], g_high[0][:, :, QUARTER:], ALU.subtract)
+        finish(res, 2, THIRD, nc.vector, nc.gpsimd)
+        gather_g(g_high[1][:, 0, :QUARTER], 3, THIRD)
+        finish_gathered(third[1][:, 1:2, :], g_high[1][:, :, :QUARTER], 3, THIRD, nc.scalar, nc.vector)
+        g_last = tile("g_last", [P, 1, QUARTER], F32, G_HIGH)
+        gather_g(g_last[:, 0, :], 3, FOURTH)
+        finish_gathered(fourth[1][:, 1:2, :], g_last[:], 3, FOURTH, nc.scalar, nc.vector)

@@ -48,7 +48,7 @@ def tile_list_pseudo_huber_reprojection_kernel(tc, tab_words, tab_scales, offs, 
             return offsets[:, j0 // 16 : j1 // 16]
 
         scale_win = tile("scale_win", [P, T // 4], I32)
-        nc.gpsimd.memset(scale_win[:], 0)
+        nc.vector.memset(scale_win[:], 0)
         w4s_raw = tile("w4s_raw", [P, KP, H // 4], I32, W4_SCALES)
         nc.vector.memset(w4s_raw[:], 0)
         moves = [(1, 0, QUARTER), (2, 0, S), (1, QUARTER, S)]
@@ -73,12 +73,12 @@ def tile_list_pseudo_huber_reprojection_kernel(tc, tab_words, tab_scales, offs, 
         load_tab(0)
         for q in range(4):
             load_tab_scales(nc.scalar if q < 2 else nc.sync, q)
+        w4_first = tile("w4_first", [P, H // 2], I32, W4_FIRST)
         for q in range(4):
             load_w4_scales(nc.scalar, q)
             if q == 1:
-                nc.scalar.activation(out=one[:], in_=unit[:], func=ACT.Sqrt)
-        w4_first = tile("w4_first", [P, H // 2], I32, W4_FIRST)
-        nc.sync.dma_start(w4_first[:], w4_words[0].bitcast(I32))
+                nc.scalar.dma_start(w4_first[:], w4_words[0].bitcast(I32))
+        nc.scalar.activation(out=one[:], in_=unit[:], func=ACT.Sqrt)
         w4_rest = [tile("w4_rest%d" % a, [P, H // 2], I32) for a in range(1, KP)]
         nc.sync.dma_start(w4_rest[0][:], w4_words[1].bitcast(I32))
         load_tab(1)

@@ -20,7 +20,8 @@ P = 128
 KP = K // 512
 HP = H // 512
 NT = N // P
-MOVE_ROWS = 112
+ALL_ROWS = ((0, 100),)
+PAIRED_ROWS = ((0, 36), (64, 100))
 HALF = S // 2
 QUARTER = S // 4
 THIRD, FOURTH = HALF, HALF + QUARTER
@@ -101,9 +102,10 @@ def tile_list_pseudo_huber_reprojection_kernel(tc, tab_words, tab_scales, offs, 
         def gather_scales(j0, j1):
             nc.vector.tensor_copy(v_scales[:, j0:j1], scale_win[:].bitcast(U8).indirect(picks(j0, j1)))
 
-        def move_scales(i):
+        def move_scales(i, runs):
             a, j0, j1 = moves[i]
-            nc.sync.dma_start(moved[i][0:MOVE_ROWS, :], v_scales[4 * a : 4 * a + MOVE_ROWS, j0:j1].bitcast(I32))
+            for r0, r1 in runs:
+                nc.sync.dma_start(moved[i][r0:r1, :], v_scales[4 * a + r0 : 4 * a + r1, j0:j1].bitcast(I32))
 
         def v_plane(a, j):
             if a == 0:
@@ -115,14 +117,14 @@ def tile_list_pseudo_huber_reprojection_kernel(tc, tab_words, tab_scales, offs, 
 
         gather_tab(0, 0, QUARTER)
         gather_scales(0, QUARTER)
-        move_scales(0)
+        move_scales(0, ALL_ROWS)
         load_tab(2)
         gather_scales(QUARTER, S)
         gather_tab(0, QUARTER, HALF, W4_FIRST + 64)
         gather_tab(0, HALF, S, W4_FIRST + KIB + 64)
-        move_scales(1)
+        move_scales(1, PAIRED_ROWS)
         nc.sync.dma_start(w4_rest[1][:], w4_words[2].bitcast(I32))
-        move_scales(2)
+        move_scales(2, ALL_ROWS)
         w4_codes = [tile("w4_codes%d" % a, [P, H // 2], I32, (None, W4_SCALES, W4_SCALES + 2 * KIB)[a]) for a in range(KP)]
         plane_first = tile("plane_first", [P, H // 4], I32)
         planes_rest = tile("planes_rest", [P, KP - 1, H // 4], I32, W4_FIRST - 2 * KIB + 64)

@@ -20,12 +20,12 @@ P = 128
 KP = K // 512
 HP = H // 512
 NT = N // P
-ALL_ROWS = ((0, 100),)
-PAIRED_ROWS = ((0, 36), (64, 100))
 HALF = S // 2
 QUARTER = S // 4
 THIRD, FOURTH = HALF, HALF + QUARTER
+PARKED = {1: 4, 2: 68}
 KIB = 1024
+COPY_OF_P, LAST_H, W2_RAW, G_HIGH = 0, 2 * KIB, (14 * KIB, 4 * KIB), 12 * KIB
 
 
 def tile_list_pseudo_huber_reprojection_kernel(tc, tab_words, tab_scales, offs, w4_words, w4_scales, w2, gT, out):
@@ -40,8 +40,6 @@ def tile_list_pseudo_huber_reprojection_kernel(tc, tab_words, tab_scales, offs, 
                 return held.tile(shape, dtype, name=name, align_bytes=64)
             return shared.tile(shape, dtype, name=name, offset=offset, align_bytes=64)
 
-        COPY_OF_P, LAST_H, W4_SCALES, W4_FIRST, W2_RAW, G_HIGH = 0, 2 * KIB, 4 * KIB, 10 * KIB, 14 * KIB, 22 * KIB
-
         offsets = held.tile([P, S // 16], U16, name="offsets")
         nc.sync.dma_start(offsets[:], offs)
 
@@ -49,101 +47,63 @@ def tile_list_pseudo_huber_reprojection_kernel(tc, tab_words, tab_scales, offs, 
             return offsets[:, j0 // 16 : j1 // 16]
 
         scale_win = tile("scale_win", [P, T // 4], I32)
-        nc.vector.memset(scale_win[:], 0)
-        w4s_raw = tile("w4s_raw", [P, KP, H // 4], I32, W4_SCALES)
+        nc.gpsimd.memset(scale_win[:, : T // 8], 0)
+        nc.vector.memset(scale_win[:, T // 8 :], 0)
+        w4s_raw = tile("w4s_raw", [P, KP, H // 4], I32)
         nc.vector.memset(w4s_raw[:], 0)
-        moves = [(1, 0, QUARTER), (2, 0, S), (1, QUARTER, S)]
-        moved = [tile("moved%d" % i, [P, (j1 - j0) // 4], I32) for i, (a, j0, j1) in enumerate(moves)]
-        for plane in moved:
-            nc.vector.memset(plane[:], 0)
+        moved = {a: tile("moved%d" % a, [P, S // 4], I32) for a in PARKED}
+        for a in PARKED:
+            nc.vector.memset(moved[a][:], 0)
         unit = tile("unit", [P, 1], F32)
         nc.vector.memset(unit[:], 1.0)
         one = tile("one", [P, 1], F32)
+
+        for a, queue in ((1, nc.sync), (2, nc.scalar)):
+            queue.dma_start(scale_win[PARKED[a] : PARKED[a] + 16, :], tab_scales[a].bitcast(I32))
+        for q in range(4):
+            queue = nc.sync if q < 2 else nc.scalar
+            queue.dma_start(scale_win[32 * q : 32 * q + 4, :], tab_scales[0, 4 * q : 4 * q + 4, :].bitcast(I32))
 
         tab_win = [tile("tab%d" % a, [P, T], I32) for a in range(KP)]
 
         def load_tab(a):
             nc.sync.dma_start(tab_win[a][:], tab_words[a].rearrange("p t i -> p (t i)").bitcast(I32))
 
-        def load_tab_scales(queue, q):
-            queue.dma_start(scale_win[32 * q : 32 * q + 4 * KP, :], tab_scales[:, 4 * q : 4 * q + 4, :].bitcast(I32))
-
-        def load_w4_scales(queue, q):
-            queue.dma_start(w4s_raw[32 * q : 32 * q + 4, :, :], w4_scales[:, 4 * q : 4 * q + 4, :].rearrange("a r c -> r a c").bitcast(I32))
-
         load_tab(0)
-        for q in range(4):
-            load_tab_scales(nc.scalar if q < 2 else nc.sync, q)
-        w4_first = tile("w4_first", [P, H // 2], I32, W4_FIRST)
-        for q in range(4):
-            load_w4_scales(nc.scalar, q)
-            if q == 1:
-                nc.scalar.dma_start(w4_first[:], w4_words[0].bitcast(I32))
+        w4_first = tile("w4_first", [P, HP, 256], I32)
+        nc.sync.dma_start(w4_first[:].rearrange("p b c -> p (b c)"), w4_words[0].bitcast(I32))
         nc.scalar.activation(out=one[:], in_=unit[:], func=ACT.Sqrt)
-        w4_rest = [tile("w4_rest%d" % a, [P, H // 2], I32) for a in range(1, KP)]
-        nc.sync.dma_start(w4_rest[0][:], w4_words[1].bitcast(I32))
+        for q in range(4):
+            nc.sync.dma_start(w4s_raw[32 * q : 32 * q + 4, :, :], w4_scales[:, 4 * q : 4 * q + 4, :].rearrange("a r c -> r a c").bitcast(I32))
+        w4_rest = [tile("w4_rest%d" % b, [P, KP - 1, 256], I32) for b in range(HP)]
+
+        def load_w4_rest(b):
+            nc.sync.dma_start(w4_rest[b][:], w4_words[1:, :, KIB * b : KIB * (b + 1)].rearrange("a p c -> p a c").bitcast(I32))
+
         load_tab(1)
-
-        v_tiles = []
-
-        def gather_tab(a, j0, j1, offset=None):
-            picked = tile("v%d_%d" % (a, j0), [P, j1 - j0], U32, offset)
-            v_tiles.append((a, j0, j1, picked))
-            nc.vector.tensor_copy(picked[:], tab_win[a][:].bitcast(U32).indirect(picks(j0, j1)))
-
-        def v_cols(a, j0, j1):
-            for pass_, lo, hi, picked in v_tiles:
-                if pass_ == a and lo <= j0 and j1 <= hi:
-                    return picked[:, j0 - lo : j1 - lo]
-            raise ValueError("no tile")
+        load_w4_rest(0)
 
         v_scales = tile("v_scales", [P, S], U8)
+        nc.vector.tensor_copy(v_scales[:], scale_win[:].bitcast(U8).indirect(offsets[:]))
 
-        def gather_scales(j0, j1):
-            nc.vector.tensor_copy(v_scales[:, j0:j1], scale_win[:].bitcast(U8).indirect(picks(j0, j1)))
-
-        def move_scales(i, runs):
-            a, j0, j1 = moves[i]
-            for r0, r1 in runs:
-                nc.sync.dma_start(moved[i][r0:r1, :], v_scales[4 * a + r0 : 4 * a + r1, j0:j1].bitcast(I32))
+        def move_scales(a, quadrants=range(4)):
+            for q in quadrants:
+                row = PARKED[a] + 4 * q
+                nc.sync.dma_start(moved[a][32 * q : 32 * q + 4, :], v_scales[row : row + 4, :].bitcast(I32))
 
         def v_plane(a, j):
             if a == 0:
                 return v_scales[:, j : j + P]
-            for plane, (pass_, j0, j1) in zip(moved, moves):
-                if pass_ == a and j0 <= j < j1:
-                    return plane[:, (j - j0) // 4 : (j - j0 + P) // 4].bitcast(U8)
-            raise ValueError("no plane")
+            return moved[a][:, j // 4 : (j + P) // 4].bitcast(U8)
 
-        gather_tab(0, 0, QUARTER)
-        gather_scales(0, QUARTER)
-        move_scales(0, ALL_ROWS)
+        move_scales(1)
         load_tab(2)
-        gather_scales(QUARTER, S)
-        gather_tab(0, QUARTER, HALF, W4_FIRST + 64)
-        gather_tab(0, HALF, S, W4_FIRST + KIB + 64)
-        move_scales(1, PAIRED_ROWS)
-        nc.sync.dma_start(w4_rest[1][:], w4_words[2].bitcast(I32))
-        move_scales(2, ALL_ROWS)
-        w4_codes = [tile("w4_codes%d" % a, [P, H // 2], I32, (None, W4_SCALES, W4_SCALES + 2 * KIB)[a]) for a in range(KP)]
-        plane_first = tile("plane_first", [P, H // 4], I32)
-        planes_rest = tile("planes_rest", [P, KP - 1, H // 4], I32, W4_FIRST - 2 * KIB + 64)
-        w4_planes = [plane_first[:], planes_rest[:, 0, :], planes_rest[:, 1, :]]
+        move_scales(2, range(3))
+        load_w4_rest(1)
+        move_scales(2, [3])
 
-        def deal(dealt, raw, words):
-            nc.scalar.copy(dealt.bitcast(U32).rearrange("p (b t q w) -> p b t q w", t=4, q=16, w=words),
-                           raw.bitcast(U32).rearrange("p (b q t w) -> p b t q w", t=4, q=16, w=words))
-
-        for b in range(HP):
-            deal(w4_codes[0][:, 256 * b : 256 * (b + 1)], w4_first[:, 256 * b : 256 * (b + 1)], 4)
-            deal(plane_first[:, 128 * b : 128 * (b + 1)], w4s_raw[:, 0, 128 * b : 128 * (b + 1)], 2)
-        deal(planes_rest[:].rearrange("p a c -> p (a c)"), w4s_raw[:, 1:, :].rearrange("p a c -> p (a c)"), 2)
-        deal(w4_codes[1][:], w4_rest[0][:], 4)
-        for b in range(HP):
-            deal(w4_codes[2][:, 256 * b : 256 * (b + 1)], w4_rest[1][:, 256 * b : 256 * (b + 1)], 4)
-
-        w2_raw = [tile("w2_raw%d" % b, [P, 4, N], F32, (None, W2_RAW)[b]) for b in range(HP)]
         w2_rows = w2.rearrange("(b q t i) n -> b t q i n", b=HP, q=16, t=4)
+        w2_raw = [tile("w2_raw%d" % b, [P, 4, N], F32, W2_RAW[b]) for b in range(HP)]
         for b in range(HP):
             for t in range(4):
                 nc.sync.dma_start(w2_raw[b][:, t, :], w2_rows[b, t])
@@ -151,21 +111,55 @@ def tile_list_pseudo_huber_reprojection_kernel(tc, tab_words, tab_scales, offs, 
         for m in range(NT):
             nc.sync.dma_start(g_win[m][:], gT[P * m : P * (m + 1), :])
 
+        def deal(dealt, raw, words):
+            nc.scalar.copy(dealt.bitcast(U32).rearrange("p (b t q w) -> p b t q w", t=4, q=16, w=words),
+                           raw.bitcast(U32).rearrange("p (b q t w) -> p b t q w", t=4, q=16, w=words))
+
+        plane_first = tile("plane_first", [P, H // 4], I32)
+        codes_first = [tile("codes_first%d" % b, [P, 256], I32) for b in range(HP)]
+        for b in range(HP):
+            deal(codes_first[b][:], w4_first[:, b, :], 4)
+            deal(plane_first[:, 128 * b : 128 * (b + 1)], w4s_raw[:, 0, 128 * b : 128 * (b + 1)], 2)
+        planes_rest = tile("planes_rest", [P, KP - 1, H // 4], I32)
+        deal(planes_rest[:].rearrange("p a c -> p (a c)"), w4s_raw[:, 1:, :].rearrange("p a c -> p (a c)"), 2)
+        codes_rest = [tile("codes_rest%d" % b, [P, KP - 1, 256], I32) for b in range(HP)]
+        deal(codes_rest[0][:].rearrange("p a c -> p (a c)"), w4_rest[0][:].rearrange("p a c -> p (a c)"), 4)
+        for a in range(KP - 1):
+            deal(codes_rest[1][:, a, :], w4_rest[1][:, a, :], 4)
+
+        def w4_slice(a, b, t):
+            codes = codes_first[b][:] if a == 0 else codes_rest[b][:, a - 1, :]
+            plane = plane_first[:] if a == 0 else planes_rest[:, a - 1, :]
+            return (codes[:, 64 * t : 64 * (t + 1)].bitcast(U8).bitcast(FP4X4),
+                    plane[:, 128 * b + 32 * t : 128 * b + 32 * (t + 1)].bitcast(U8))
+
+        v_tiles = []
+
+        def gather_tab(a, j0, j1):
+            picked = tile("v%d_%d" % (a, j0), [P, j1 - j0], U32)
+            v_tiles.append((a, j0, j1, picked))
+            nc.vector.tensor_copy(picked[:], tab_win[a][:].bitcast(U32).indirect(picks(j0, j1)))
+
+        def v_cols(a, j):
+            for pass_, lo, hi, picked in v_tiles:
+                if pass_ == a and lo <= j < hi:
+                    return picked[:, j - lo : j - lo + P]
+            raise ValueError("no tile")
+
+        for a, cuts in enumerate(((0, QUARTER, HALF, S), (0, HALF, S), (0, QUARTER, HALF, S))):
+            for j0, j1 in zip(cuts, cuts[1:]):
+                gather_tab(a, j0, j1)
+
         def bank_tile(shape, bank):
             return psum.tile(shape, F32, name="bank", tag="bank%d" % bank)
 
         def decode_passes(bank, b, j, passes):
             for a in passes:
                 for t in range(4):
-                    nc.tensor.matmul_mx(
-                        out=bank[:, t, :],
-                        lhsT=w4_codes[a][:, 256 * b + 64 * t : 256 * b + 64 * (t + 1)].bitcast(U8).bitcast(FP4X4),
-                        lhsT_scale=w4_planes[a][:, 128 * b + 32 * t : 128 * b + 32 * (t + 1)].bitcast(U8),
-                        rhs=v_cols(a, j, j + P).bitcast(FP8X4),
-                        rhs_scale=v_plane(a, j),
-                        start=(a == 0 and t == 0),
-                        stop=(a == KP - 1 and t == 3),
-                    )
+                    codes, plane = w4_slice(a, b, t)
+                    nc.tensor.matmul_mx(out=bank[:, t, :], lhsT=codes, lhsT_scale=plane,
+                                        rhs=v_cols(a, j).bitcast(FP8X4), rhs_scale=v_plane(a, j),
+                                        start=(a == 0 and t == 0), stop=(a == KP - 1 and t == 3))
 
         def relu(grouped, bank, j):
             lo = j % grouped.shape[1]
@@ -180,18 +174,17 @@ def tile_list_pseudo_huber_reprojection_kernel(tc, tab_words, tab_scales, offs, 
                                   in_=grouped[:].rearrange("p j t -> p (j t)"))
             return codes
 
-        early = [(b, j0 + j) for j0 in (0, QUARTER) for b in range(HP) for j in (0, P)]
-        early_banks = [bank_tile([P, 4, P], i) for i in range(8)]
-        for bank, (b, j) in zip(early_banks, early):
-            decode_passes(bank, b, j, [0])
-        gather_tab(1, 0, QUARTER)
-        gather_tab(1, QUARTER, S)
-        for j0, j1 in ((0, QUARTER), (QUARTER, HALF), (HALF, S)):
-            gather_tab(2, j0, j1)
+        early = [[bank_tile([P, 4, P], 4 * b + i) for i in range(4)] for b in range(HP)]
+        for b in range(HP):
+            for i in range(4):
+                decode_passes(early[b][i], b, P * i, [0])
+        for i in range(4):
+            decode_passes(early[0][i], 0, P * i, [1])
         first_h = [tile("first_h%d" % b, [P, HALF, 4], BF16) for b in range(HP)]
-        for bank, (b, j) in zip(early_banks, early):
-            decode_passes(bank, b, j, [1, 2])
-            relu(first_h[b], bank, j)
+        for b in range(HP):
+            for i in range(4):
+                decode_passes(early[b][i], b, P * i, [2] if b == 0 else [1, 2])
+                relu(first_h[b], early[b][i], P * i)
 
         w2_codes = [tile("w2_codes%d" % b, [P, N], U32) for b in range(HP)]
         w2_scales = tile("w2_scales", [P, HP, N], U8)
@@ -212,10 +205,10 @@ def tile_list_pseudo_huber_reprojection_kernel(tc, tab_words, tab_scales, offs, 
         round_w2(0)
         for cols in halves:
             quantize_w2(0, cols)
-        first_codes = [quantize_h(first_h[0], 0, 0)]
+        first_codes = [quantize_h(first_h[0], 0, 0, W2_RAW[0])]
         round_w2(1)
         quantize_w2(1, halves[0])
-        first_codes.append(quantize_h(first_h[1], 1, 0, W2_RAW))
+        first_codes.append(quantize_h(first_h[1], 1, 0, W2_RAW[1]))
         quantize_w2(1, halves[1])
 
         def project(bank, rows, j0, codes, passes):
@@ -266,6 +259,7 @@ def tile_list_pseudo_huber_reprojection_kernel(tc, tab_words, tab_scales, offs, 
         decode(third_h[0], 0, THIRD, 0)
         decode(third_h[0], 0, THIRD + P, 1)
         decode(third_h[1], 1, THIRD, 6)
+        decode(third_h[1], 1, THIRD + P, 7)
         first_banks = [bank_tile([P, 1, HALF], 2 + m) for m in range(NT)]
         first = []
         for m in range(NT):
@@ -277,15 +271,14 @@ def tile_list_pseudo_huber_reprojection_kernel(tc, tab_words, tab_scales, offs, 
         g_low = tile("g_low", [P, 2, HALF], F32)
         gather_g(g_low[:, 0, :], 0, HALF)
         finish_fused(0)
-        decode(third_h[1], 1, THIRD + P, 2)
         finish_fused(1)
         gather_g(g_low[:, 1, :], 1, HALF)
         third_codes = [quantize_h(third_h[b], b, THIRD, COPY_OF_P + KIB * b) for b in range(HP)]
         fourth_h = [tile("h%d_%d" % (b, FOURTH), [P, QUARTER, 4], BF16, (None, LAST_H)[b]) for b in range(HP)]
-        decode(fourth_h[0], 0, FOURTH, 3)
-        decode(fourth_h[0], 0, FOURTH + P, 4)
-        decode(fourth_h[1], 1, FOURTH, 5)
-        decode(fourth_h[1], 1, FOURTH + P, 2)
+        decode(fourth_h[0], 0, FOURTH, 2)
+        decode(fourth_h[0], 0, FOURTH + P, 3)
+        decode(fourth_h[1], 1, FOURTH, 4)
+        decode(fourth_h[1], 1, FOURTH + P, 5)
         third = [bank_tile([P, 2, QUARTER], i) for i in range(2)]
         for i in range(2):
             project(third[i], [2 * i, 2 * i + 1], THIRD, third_codes, range(HP))

from contextlib import ExitStack

import concourse.mybir as mybir

K, T, S, H, N = 1536, 2048, 1024, 1024, 512
FLOPS = 2 * K * H * S + 2 * H * N * S

F32 = mybir.dt.float32
BF16 = mybir.dt.bfloat16
I32 = mybir.dt.int32
U32 = mybir.dt.uint32
U16 = mybir.dt.uint16
U8 = mybir.dt.uint8
FP8X4 = mybir.dt.float8_e4m3fn_x4
FP4X4 = mybir.dt.float4_e2m1fn_x4
ACT = mybir.ActivationFunctionType
ALU = mybir.AluOpType

P = 128
KP = K // 512
HP = H // 512
NT = N // P
HALF = S // 2
QUARTER = S // 4
THIRD, FOURTH = HALF, HALF + QUARTER
PARKED = {1: 4, 2: 68}
KIB = 1024
COPY_OF_P, LAST_H, W2_RAW, G_HIGH = 0, 2 * KIB, (14 * KIB, 4 * KIB), 12 * KIB


def tile_list_pseudo_huber_reprojection_kernel(tc, tab_words, tab_scales, offs, w4_words, w4_scales, w2, gT, out):
    nc = tc.nc
    with ExitStack() as ctx:
        held = ctx.enter_context(tc.tile_pool(name="held", bufs=1))
        shared = ctx.enter_context(tc.tile_pool(name="shared", bufs=1))
        psum = ctx.enter_context(tc.psum_pool(name="psum", bufs=1))

        def tile(name, shape, dtype, offset=None):
            if offset is None:
                return held.tile(shape, dtype, name=name, align_bytes=64)
            return shared.tile(shape, dtype, name=name, offset=offset, align_bytes=64)

        offsets = held.tile([P, S // 16], U16, name="offsets")
        nc.sync.dma_start(offsets[:], offs)

        def picks(j0, j1):
            return offsets[:, j0 // 16 : j1 // 16]

        scale_win = tile("scale_win", [P, T // 4], I32)
        nc.gpsimd.memset(scale_win[:, : T // 8], 0)
        nc.vector.memset(scale_win[:, T // 8 :], 0)
        w4s_raw = tile("w4s_raw", [P, KP, H // 4], I32)
        nc.vector.memset(w4s_raw[:], 0)
        moved = {a: tile("moved%d" % a, [P, S // 4], I32) for a in PARKED}
        for a in PARKED:
            nc.vector.memset(moved[a][:], 0)
        unit = tile("unit", [P, 1], F32)
        nc.vector.memset(unit[:], 1.0)
        one = tile("one", [P, 1], F32)

        for a, queue in ((1, nc.sync), (2, nc.scalar)):
            queue.dma_start(scale_win[PARKED[a] : PARKED[a] + 16, :], tab_scales[a].bitcast(I32))
        for q in range(4):
            queue = nc.sync if q < 2 else nc.scalar
            queue.dma_start(scale_win[32 * q : 32 * q + 4, :], tab_scales[0, 4 * q : 4 * q + 4, :].bitcast(I32))

        tab_win = [tile("tab%d" % a, [P, T], I32) for a in range(KP)]

        def load_tab(a):
            nc.sync.dma_start(tab_win[a][:], tab_words[a].rearrange("p t i -> p (t i)").bitcast(I32))

        load_tab(0)
        w4_first = tile("w4_first", [P, HP, 256], I32)
        nc.sync.dma_start(w4_first[:].rearrange("p b c -> p (b c)"), w4_words[0].bitcast(I32))
        nc.scalar.activation(out=one[:], in_=unit[:], func=ACT.Sqrt)
        for q in range(4):
            nc.sync.dma_start(w4s_raw[32 * q : 32 * q + 4, :, :], w4_scales[:, 4 * q : 4 * q + 4, :].rearrange("a r c -> r a c").bitcast(I32))
        w4_rest = [tile("w4_rest%d" % b, [P, KP - 1, 256], I32) for b in range(HP)]

        def load_w4_rest(b):
            nc.sync.dma_start(w4_rest[b][:], w4_words[1:, :, KIB * b : KIB * (b + 1)].rearrange("a p c -> p a c").bitcast(I32))

        load_tab(1)
        load_w4_rest(0)

        v_scales = tile("v_scales", [P, S], U8)
        nc.vector.tensor_copy(v_scales[:], scale_win[:].bitcast(U8).indirect(offsets[:]))

        def move_scales(a, quadrants=range(4)):
            for q in quadrants:
                row = PARKED[a] + 4 * q
                nc.sync.dma_start(moved[a][32 * q : 32 * q + 4, :], v_scales[row : row + 4, :].bitcast(I32))

        def v_plane(a, j):
            if a == 0:
                return v_scales[:, j : j + P]
            return moved[a][:, j // 4 : (j + P) // 4].bitcast(U8)

        move_scales(1)
        load_tab(2)
        move_scales(2, range(3))
        load_w4_rest(1)
        move_scales(2, [3])

        w2_rows = w2.rearrange("(b q t i) n -> b t q i n", b=HP, q=16, t=4)
        w2_raw = [tile("w2_raw%d" % b, [P, 4, N], F32, W2_RAW[b]) for b in range(HP)]
        for b in range(HP):
            for t in range(4):
                nc.sync.dma_start(w2_raw[b][:, t, :], w2_rows[b, t])
        g_win = [tile("g_win%d" % m, [P, T], F32) for m in range(NT)]
        for m in range(NT):
            nc.sync.dma_start(g_win[m][:], gT[P * m : P * (m + 1), :])

        def deal(dealt, raw, words):
            nc.scalar.copy(dealt.bitcast(U32).rearrange("p (b t q w) -> p b t q w", t=4, q=16, w=words),
                           raw.bitcast(U32).rearrange("p (b q t w) -> p b t q w", t=4, q=16, w=words))

        plane_first = tile("plane_first", [P, H // 4], I32)
        codes_first = [tile("codes_first%d" % b, [P, 256], I32) for b in range(HP)]
        for b in range(HP):
            deal(codes_first[b][:], w4_first[:, b, :], 4)
            deal(plane_first[:, 128 * b : 128 * (b + 1)], w4s_raw[:, 0, 128 * b : 128 * (b + 1)], 2)
        planes_rest = tile("planes_rest", [P, KP - 1, H // 4], I32)
        deal(planes_rest[:].rearrange("p a c -> p (a c)"), w4s_raw[:, 1:, :].rearrange("p a c -> p (a c)"), 2)
        codes_rest = [tile("codes_rest%d" % b, [P, KP - 1, 256], I32) for b in range(HP)]
        deal(codes_rest[0][:].rearrange("p a c -> p (a c)"), w4_rest[0][:].rearrange("p a c -> p (a c)"), 4)
        for a in range(KP - 1):
            deal(codes_rest[1][:, a, :], w4_rest[1][:, a, :], 4)

        def w4_slice(a, b, t):
            codes = codes_first[b][:] if a == 0 else codes_rest[b][:, a - 1, :]
            plane = plane_first[:] if a == 0 else planes_rest[:, a - 1, :]
            return (codes[:, 64 * t : 64 * (t + 1)].bitcast(U8).bitcast(FP4X4),
                    plane[:, 128 * b + 32 * t : 128 * b + 32 * (t + 1)].bitcast(U8))

        v_tiles = []

        def gather_tab(a, j0, j1):
            picked = tile("v%d_%d" % (a, j0), [P, j1 - j0], U32)
            v_tiles.append((a, j0, j1, picked))
            nc.vector.tensor_copy(picked[:], tab_win[a][:].bitcast(U32).indirect(picks(j0, j1)))

        def v_cols(a, j):
            for pass_, lo, hi, picked in v_tiles:
                if pass_ == a and lo <= j < hi:
                    return picked[:, j - lo : j - lo + P]
            raise ValueError("no tile")

        for a, cuts in enumerate(((0, QUARTER, HALF, S), (0, HALF, S), (0, QUARTER, HALF, S))):
            for j0, j1 in zip(cuts, cuts[1:]):
                gather_tab(a, j0, j1)

        def bank_tile(shape, bank):
            return psum.tile(shape, F32, name="bank", tag="bank%d" % bank)

        def decode_passes(bank, b, j, passes):
            for a in passes:
                for t in range(4):
                    codes, plane = w4_slice(a, b, t)
                    nc.tensor.matmul_mx(out=bank[:, t, :], lhsT=codes, lhsT_scale=plane,
                                        rhs=v_cols(a, j).bitcast(FP8X4), rhs_scale=v_plane(a, j),
                                        start=(a == 0 and t == 0), stop=(a == KP - 1 and t == 3))

        def relu(grouped, bank, j):
            lo = j % grouped.shape[1]
            nc.scalar.activation(out=grouped[:, lo : lo + P, :], in_=bank[:].rearrange("p t j -> p j t"), func=ACT.Relu)

        h_scales = tile("h_scales", [P, HP, S], U8)

        def quantize_h(grouped, b, j0, offset=None):
            width = grouped.shape[1]
            codes = tile("h_codes%d_%d" % (b, j0), [P, width], U32, offset)
            nc.vector.quantize_mx(out=codes[:].bitcast(FP8X4), scales=h_scales[:, b, j0 : j0 + width],
                                  in_=grouped[:].rearrange("p j t -> p (j t)"))
            return codes

        early = [[bank_tile([P, 4, P], 4 * b + i) for i in range(4)] for b in range(HP)]
        for b in range(HP):
            for i in range(4):
                decode_passes(early[b][i], b, P * i, [0])
        for i in range(4):
            decode_passes(early[0][i], 0, P * i, [1])
        first_h = [tile("first_h%d" % b, [P, HALF, 4], BF16) for b in range(HP)]
        for b in range(HP):
            for i in range(4):
                decode_passes(early[b][i], b, P * i, [2] if b == 0 else [1, 2])
                relu(first_h[b], early[b][i], P * i)

        w2_codes = [tile("w2_codes%d" % b, [P, N], U32) for b in range(HP)]
        w2_scales = tile("w2_scales", [P, HP, N], U8)

        w2_rounded = [tile("w2_rounded%d" % b, [P, N, 4], BF16) for b in range(HP)]

        halves = (slice(0, N // 2), slice(N // 2, N))

        def round_w2(b):
            for cols in halves:
                nc.vector.tensor_copy(w2_rounded[b][:, cols, :].rearrange("p (c i) t -> p c t i", i=4),
                                      w2_raw[b][:, :, cols].rearrange("p t (c i) -> p c t i", i=4))

        def quantize_w2(b, cols):
            nc.vector.quantize_mx(out=w2_codes[b][:, cols].bitcast(FP8X4), scales=w2_scales[:, b, cols],
                                  in_=w2_rounded[b][:, cols, :].rearrange("p n t -> p (n t)"))

        round_w2(0)
        for cols in halves:
            quantize_w2(0, cols)
        first_codes = [quantize_h(first_h[0], 0, 0, W2_RAW[0])]
        round_w2(1)
        quantize_w2(1, halves[0])
        first_codes.append(quantize_h(first_h[1], 1, 0, W2_RAW[1]))
        quantize_w2(1, halves[1])

        def project(bank, rows, j0, codes, passes):
            width = bank.shape[2]
            for b in passes:
                for i, m in enumerate(rows):
                    nc.tensor.matmul_mx(
                        out=bank[:, i, :],
                        lhsT=w2_codes[b][:, P * m : P * (m + 1)].bitcast(FP8X4),
                        lhsT_scale=w2_scales[:, b, P * m : P * (m + 1)],
                        rhs=codes[b][:].bitcast(FP8X4),
                        rhs_scale=h_scales[:, b, j0 : j0 + width],
                        start=(b == 0 and i == 0),
                        stop=(b == HP - 1 and i == len(rows) - 1),
                    )

        def decode(grouped, b, j, number):
            bank = bank_tile([P, 4, P], number)
            decode_passes(bank, b, j, range(KP))
            relu(grouped, bank, j)

        out_rows = out.rearrange("(m p) j -> p m j", p=P)

        def finish(res, m0, j0, square, minus_one):
            rows, width = res.shape[1], res.shape[2]
            if square is nc.scalar:
                nc.scalar.activation(out=res[:], in_=res[:], func=ACT.Square)
            else:
                square.tensor_tensor(res[:], res[:], res[:], ALU.mult)
            nc.scalar.activation(out=res[:], in_=res[:], func=ACT.Sqrt, bias=one[:])
            minus_one.tensor_scalar(res[:], res[:], 1.0, -1.0, ALU.mult, ALU.add)
            nc.sync.dma_start(out_rows[:, m0 : m0 + rows, j0 : j0 + width], res[:])

        def finish_fused(m):
            res = tile("res%d" % m, [P, 1, HALF], F32)
            nc.vector.tensor_tensor(res[:, 0, :], g_win[m][:].indirect(picks(0, HALF)), first[m][:], ALU.subtract)
            finish(res, m, 0, nc.scalar, nc.gpsimd)

        def finish_gathered(predicted, observed, m0, j0, square, minus_one, offset=None):
            res = tile("res%d_%d" % (m0, j0), list(predicted.shape), F32, offset)
            nc.vector.tensor_tensor(res[:], predicted, observed, ALU.subtract)
            finish(res, m0, j0, square, minus_one)

        def gather_g(picked, m, j0):
            nc.vector.tensor_copy(picked, g_win[m][:].indirect(picks(j0, j0 + picked.shape[1])))

        third_h = [tile("h%d_%d" % (b, THIRD), [P, QUARTER, 4], BF16) for b in range(HP)]
        decode(third_h[0], 0, THIRD, 0)
        decode(third_h[0], 0, THIRD + P, 1)
        decode(third_h[1], 1, THIRD, 6)
        decode(third_h[1], 1, THIRD + P, 7)
        first_banks = [bank_tile([P, 1, HALF], 2 + m) for m in range(NT)]
        first = []
        for m in range(NT):
            project(first_banks[m], [m], 0, first_codes, range(HP))
            predicted = tile("p%d" % m, [P, HALF], F32, COPY_OF_P if m == 1 else None)
            nc.scalar.copy(predicted[:], first_banks[m][:, 0, :])
            first.append(predicted)

        g_low = tile("g_low", [P, 2, HALF], F32)
        gather_g(g_low[:, 0, :], 0, HALF)
        finish_fused(0)
        finish_fused(1)
        gather_g(g_low[:, 1, :], 1, HALF)
        third_codes = [quantize_h(third_h[b], b, THIRD, COPY_OF_P + KIB * b) for b in range(HP)]
        fourth_h = [tile("h%d_%d" % (b, FOURTH), [P, QUARTER, 4], BF16, (None, LAST_H)[b]) for b in range(HP)]
        decode(fourth_h[0], 0, FOURTH, 2)
        decode(fourth_h[0], 0, FOURTH + P, 3)
        decode(fourth_h[1], 1, FOURTH, 4)
        decode(fourth_h[1], 1, FOURTH + P, 5)
        third = [bank_tile([P, 2, QUARTER], i) for i in range(2)]
        for i in range(2):
            project(third[i], [2 * i, 2 * i + 1], THIRD, third_codes, range(HP))
        finish_fused(2)
        g_high = [tile("g_high%d" % i, [P, 1, HALF], F32, (G_HIGH, LAST_H)[i]) for i in range(2)]
        gather_g(g_high[0][:, 0, :], 2, HALF)
        fourth_codes = [quantize_h(fourth_h[b], b, FOURTH) for b in range(HP)]
        fourth = [bank_tile([P, 2, QUARTER], 6 + i) for i in range(2)]
        for b in range(HP):
            for i in range(2):
                project(fourth[i], [2 * i, 2 * i + 1], FOURTH, fourth_codes, [b])
        finish_gathered(third[0][:], g_low[:, :, :QUARTER], 0, THIRD, nc.scalar, nc.gpsimd)
        finish_fused(3)
        finish_gathered(fourth[0][:], g_low[:, :, QUARTER:], 0, FOURTH, nc.scalar, nc.gpsimd)
        res = tile("res_high", [P, 1, HALF], F32)
        nc.vector.tensor_tensor(res[:, :, :QUARTER], third[1][:, 0:1, :], g_high[0][:, :, :QUARTER], ALU.subtract)
        nc.vector.tensor_tensor(res[:, :, QUARTER:], fourth[1][:, 0:1, :], g_high[0][:, :, QUARTER:], ALU.subtract)
        finish(res, 2, THIRD, nc.vector, nc.gpsimd)
        gather_g(g_high[1][:, 0, :QUARTER], 3, THIRD)
        finish_gathered(third[1][:, 1:2, :], g_high[1][:, :, :QUARTER], 3, THIRD, nc.scalar, nc.vector)
        g_last = tile("g_last", [P, 1, QUARTER], F32, G_HIGH)
        gather_g(g_last[:, 0, :], 3, FOURTH)
        finish_gathered(fourth[1][:, 1:2, :], g_last[:], 3, FOURTH, nc.scalar, nc.vector)
